import numpy as np, ml_dtypes
CORES = [1,5,17,21,33,37,49,53]
N = 8
BF = ml_dtypes.bfloat16
def f(rng, *shape):
    return (rng.standard_normal(shape, dtype=np.float32) * np.exp2(rng.integers(-2, 3, shape[:-1] + (1,)))).astype(BF)
def wide(rng, *shape):
    v = f(rng, *shape).astype(np.float32); k = shape[:-2] + (1, shape[-1])
    return (v * np.exp2(rng.integers(-6, 7, k)) * (rng.random(k) > 0.0625)).astype(BF)
def gentries(a):
    return np.ascontiguousarray(a.reshape(8, 16, -1).transpose(0, 2, 1)).reshape(8, -1)
def gtable(e):
    e = np.asarray(e); return np.ascontiguousarray(e.reshape(8, -1, 16).transpose(0, 2, 1)).reshape(128, -1).astype(np.int32)
B, PI, C, F, NEED, R = 256, 8, 8, 4096, 8, 3
def faces(rng):
    v = rng.standard_normal((N, 8, 16, F), dtype=np.float32) + rng.standard_normal((N, 8, 1, F), dtype=np.float32)
    return (v * np.exp2(rng.integers(-2, 3, (N, 8, 16, 1)))).astype(BF).reshape(N, 128, F)
def parts(rng):
    return rng.integers(0, C + 1, (N, 8, PI, B)), rng.integers(0, F, (N, 8, C, PI, B)), rng.integers(0, PI, (N, 8, B))
def pack(x, c, kinds, p):
    s = np.where(np.arange(C)[:, None, None] < c[:, :, None], kinds, F)
    return {"x": x, "sd": np.stack([gtable(a.reshape(8, -1)) for a in s]), "act": np.stack([gtable(a) for a in p])}
def setup_inputs(rng):
    c, kinds, p = parts(rng)
    return pack(faces(rng), c, kinds, p)
def setup_inputs_full(rng):
    c, kinds, p = parts(rng)
    c = C - rng.choice(np.array([0, 0, 0, 1, 1, 2]), (N, 8, PI, B))
    c[:, 1:3] = C - 1; p[:, 1] = rng.integers(0, PI); p[:, 2] = rng.integers(0, PI, (N, 1)); kinds[:, 2] = rng.integers(0, F)
    n = np.take_along_axis(c, p[:, :, None, :], 2); n[..., ::2] = C; n[:, 1:3] = C
    np.put_along_axis(c, p[:, :, None, :], n, 2); c[0, 0] = C
    return pack(faces(rng), c, kinds, p)
def setup_inputs_ties(rng):
    c, kinds, p = parts(rng)
    cl = rng.choice(np.array([-1] * 7 + [0, 16 - NEED, 17 - NEED, NEED - 1, NEED, NEED + 1, 16]), (N, 8, 1, F))
    o = np.argsort(rng.random((N, 8, 16)), axis=2)[..., None]
    v = np.where(cl < 0, 1.0, np.where(o < cl, 2.0, 0.0))
    z = v[:, 1::4] - 1.0
    v[:, 1::4] = np.where(z == 0, rng.choice(np.array([0.0, -0.0]), (N, 2, 1, F)), z)
    e = rng.integers(-3, 4, (N, 8, 16, 1)); e[:, 3] = 59
    v = v * np.exp2(e)
    v[:, 2::4] = v[:, 2::4] * np.exp2(rng.choice(np.array([-57.0, 50.0]), (N, 2, 1, F)))
    c = 2 * rng.integers(0, C // 2 + 1, (N, 8, PI, B))
    return pack(v.astype(BF).reshape(N, 128, F), c, kinds, p)
def setup_inputs_sparse(rng):
    c, kinds, p = parts(rng)
    c = np.where(rng.random((N, 8, PI, B)) < 0.2, rng.integers(1, C + 1, (N, 8, PI, B)), 0)
    n = np.where(rng.random((N, 8, 1, B)) < 0.5, rng.integers(1, C + 1, (N, 8, 1, B)), 0)
    q = rng.permutation(N); n[q[0]] = 0; n[q[1]] = 1
    h = rng.permutation(8); n[:, h[1]] = 0
    np.put_along_axis(c, p[:, :, None, :], n, 2); c[:, h[0]] = 0
    return pack(faces(rng), c, kinds, p)
def setup_inputs_ends(rng):
    c, kinds, p = parts(rng); few = np.array([0, F - 1, 1, F - 2, F // 2])
    p = (PI - 1) * rng.integers(0, 2, (N, 8, B))
    kinds[:, ::2] = rng.choice(few, (N, 4, C, PI, B)); kinds[:, 0] = rng.choice(few, (1, 1, 1, B))
    return pack(faces(rng), c, kinds, p)
def setup_inputs_spread(rng):
    c, kinds, p = parts(rng)
    c = np.minimum(((C + 1) * rng.random((N, 8, PI, B)) ** np.exp2(rng.integers(-2, 3, (N, 8, 1, B)))).astype(np.int64), C)
    kinds = np.minimum((F * rng.random((N, 8, C, PI, B)) ** 3).astype(np.int64), F - 1)
    v = wide(rng, N, 128, F).astype(np.float32).reshape(N, 8, 16, F); v[:, 1::2] *= np.float32(2.0 ** 44)
    return pack(v.reshape(N, 128, F).astype(BF), c, kinds, p)
def check_inputs(d):
    bad = []
    v = np.abs(np.asarray(d["x"]).astype(np.float32))
    if not np.all((v == 0) | ((v >= 2.0 ** -60) & (v <= 2.0 ** 60))): bad.append("size of x")
    if np.min(d["sd"]) < 0 or np.max(d["sd"]) > F: bad.append("range of sd")
    if np.min(d["act"]) < 0 or np.max(d["act"]) > PI - 1: bad.append("range of act")
    s = np.stack([gentries(a) for a in d["sd"]]).reshape(N, 8, C, PI, B)
    if np.any((s[:, :, :-1] == F) & (s[:, :, 1:] != F)): bad.append("a seed above an empty slot")
    return bad
def reference(x, sd, act):
    s = np.stack([gentries(a) for a in sd]).astype(np.int64).reshape(N, 8, C, PI, B)
    p = np.stack([gentries(a) for a in act]).astype(np.int64)
    xf = np.concatenate([x.astype(np.float32).reshape(N, 8, 16, F), np.zeros((N, 8, 16, 1), np.float32)], axis=3)
    pits = np.arange(PI)[:, None]; slots = np.arange(C)[:, None, None]; score = np.zeros((N, 8, B), np.int64)
    for rnd in range(R):
        c = np.add.reduce((s != F).astype(np.int64), axis=2)
        up = np.take_along_axis(s, p[:, :, None, None, :], 3)[:, :, :, 0]
        n = np.take_along_axis(c, p[:, :, None, :], 2)[:, :, 0]
        own = pits == p[:, :, None, :]
        s = np.where(own[:, :, None], F, s); c = np.where(own, 0, c)
        up, p, n = np.roll(up, 1, axis=0), np.roll(p, 1, axis=0), np.roll(n, 1, axis=0)
        k = (pits - p[:, :, None, :] - 1) & (PI - 1)
        here = k < n[:, :, None, :]
        a = np.where(here, np.take_along_axis(up, np.minimum(k, C - 1), 2), F)
        w = np.zeros((N, 8, PI, B), np.int64)
        for r in range(N):
            fa = np.take_along_axis(xf[r], a[r].reshape(8, 1, PI * B), 2)
            for j in range(C):
                fs = np.take_along_axis(xf[r], s[r, :, j].reshape(8, 1, PI * B), 2)
                beat = np.add.reduce((fa > fs).astype(np.int64), axis=1) >= NEED
                w[r] += beat.reshape(8, PI, B) & (s[r, :, j] != F)
        cap = here & ((2 * w > c) | (c == C))
        score = score + np.add.reduce(np.where(cap, c, 0), axis=2)
        at = np.where(cap, 0, c)
        s = np.where(cap[:, :, None], F, s)
        s = np.where(here[:, :, None] & (slots == at[:, :, None]), a[:, :, None], s)
        last = (p + n) & (PI - 1)
        p = np.where(np.take_along_axis(cap, last[:, :, None, :], 2)[:, :, 0], PI - 1 - last, last)
    return {"ys": np.stack([gtable(v.reshape(8, -1)) for v in s]).astype(np.float32),
            "yp": np.stack([gtable(v) for v in p]).astype(np.float32), "yc": np.stack([gtable(v) for v in score]).astype(np.float32)}

@@ -1,0 +1,402 @@
+from concourse.bass import DstId, RemoteDMATransfer
+from concourse.mybir import AluOpType as A, ActivationFunctionType as AF
+
+F = 4096.0
+B = 8192.0
+NB = 8
+NP = 8 * NB
+WID = 16 * NP
+CH = (0, 1)
+RS = (1, 2, 3)
+CFG = {
+    "ST": {(0, 1): 2, (1, 1): 2, (0, 2): 6, (1, 2): 6, (0, 3): 6, (1, 3): 6},
+    "GV": {(0, 1), (0, 2), (1, 1)},
+    "SM": {1: "v", 2: "v", 3: "v"},
+    "XS": {(0, 2), (1, 2), (0, 3), (1, 3)},
+}
+ORDER = [22,24,21,2,1,3,6,20,0,19,4,18,23,10,28,17,30,25,37,5,26,38,11,31,29,32,33,41,40,14,27,52,53,13,15,42,16,55,51,34,39,58,35,49,50,43,64,44,36,45,57,54,65,46,78,47,59,69,63,72,68,73,9,67,62,121,74,71,76,7,8,122,56,70,113,114,77,79,84,80,126,75,66,116,81,85,82,115,60,86,87,83,129,61,128,130,88,140,89,123,92,90,91,93,94,95,97,96,98,105,104,117,118,127,132,106,144,107,119,120,108,109,131,110,142,145,141,143,136,137,148,149,124,99,138,135,133,134,139,125,48,101,150,102,103,178,146,187,179,177,186,147,151,100,111,152,196,185,153,156,154,157,155,184,197,158,198,199,160,159,161,162,168,165,166,180,170,167,181,195,191,249,200,171,169,172,201,202,112,173,208,190,189,163,204,194,193,203,175,206,209,182,210,174,192,205,188,207,214,241,212,164,243,215,244,248,260,183,211,213,176,12,216,217,261,220,218,221,222,223,225,226,224,242,250,262,219,264,232,229,245,246,251,234,255,230,254,231,263,266,235,236,233,237,265,268,227,267,252,253,259,256,269,238,270,271,305,278,272,276,258,257,274,247,239,279,307,312,228,308,275,277,273,326,280,306,281,284,282,309,328,285,315,291,283,292,287,286,327,289,288,290,293,297,329,313,314,330,332,331,333,296,294,298,322,321,318,310,299,295,334,335,300,336,344,303,301,316,323,319,320,317,337,324,371,325,342,311,340,302,338,363,364,365,372,384,240,377,386,385,373,388,376,343,387,389,341,375,374,380,390,345,339,381,392,383,346,366,391,347,393,382,378,348,398,402,399,403,350,351,379,367,355,394,357,396,395,353,352,356,304,368,354,358,369,400,370,349,397,401,404,405,359,408,406,409,410,413,411,412,414,360,415,407,417,416,418,361,419,362,420,423,421,422,424]
+
+SCRATCH = {
+    "xs": ("sbuf", [128, 4112], "bfloat16"),
+    "sdi": ("sbuf", [128, 64, 16], "int32"),
+    "acti": ("sbuf", [128, 2, NB], "int32"),
+    "st": ("sbuf", [128, 64, 16], "float32"),
+    "fill": ("sbuf", [128, 2, 8 * NP], "bfloat16"),
+    "ones": ("sbuf", [128, 128], "bfloat16"),
+    "zeros": ("sbuf", [128, 128], "bfloat16"),
+    "eye": ("sbuf", [128, 128], "bfloat16"),
+    "eyef": ("sbuf", [128, 128], "float32"),
+    "seye": ("sbuf", [128, NP], "bfloat16"),
+    "grp0": ("sbuf", [128, 8], "bfloat16"),
+    "grp": ("sbuf", [128, 8], "bfloat16"),
+    "qio": ("sbuf", [128, 8, NB], "float32"),
+    "tb": ("sbuf", [128, 4], "float32"),
+    "outp": ("sbuf", [128, 2, 16], "float32"),
+    "fa0p": ("psum", [128, 512], "float32"),
+    "fa1p": ("psum", [128, 512], "float32"),
+    "d0p": ("psum", [128, 512], "float32"),
+    "d1p": ("psum", [128, 512], "float32"),
+    "rp": ("psum", [128, 512], "float32"),
+    "wp": ("psum", [128, 64, NB], "float32"),
+    "gp": ("psum", [128, 64, NB], "float32"),
+    "vp": ("psum", [128, 64, NB], "float32"),
+}
+EYES = {"neye": -1.0, "eyeb": B, "eyeib": 1 / B, "neyeib": -1 / B, "eye64": 64.0, "eyek": 1 / 1024.0, "neyem": -1 / (8 * B)}
+for _n in EYES:
+    SCRATCH[_n] = ("sbuf", [128, 128], "bfloat16")
+for _c in CH:
+    SCRATCH["off%d" % _c] = ("sbuf", [128, 8 * NP], "uint16")
+    SCRATCH["fs%d" % _c] = ("sbuf", [128, 6 * WID], "bfloat16")
+    SCRATCH["cmp%d" % _c] = ("sbuf", [128, 8 * WID], "bfloat16")
+    SCRATCH["xf%d" % _c] = ("sbuf", [128, WID], "bfloat16")
+    SCRATCH["thr%d" % _c] = ("sbuf", [128, 512], "bfloat16")
+    SCRATCH["prod%d" % _c] = ("sbuf", [128, 64, NB], "float32")
+    SCRATCH["dead%d" % _c] = ("sbuf", [128, 5 * NP], "bfloat16")
+    SCRATCH["fin%d" % _c] = ("sbuf", [128, 2, 8, NB], "float32")
+    for _n in ("here", "e8", "ncap", "y"):
+        SCRATCH["%s%d" % (_n, _c)] = ("sbuf", [128, 8, NB], "bfloat16")
+    for _n in ("t", "tmp", "xk", "s6"):
+        SCRATCH["%s%d" % (_n, _c)] = ("sbuf", [128, 8, NB], "float32")
+    for _r in RS:
+        SCRATCH["fa%d%d" % (_c, _r)] = ("sbuf", [128, WID], "bfloat16")
+        SCRATCH["sa%d%d" % (_c, _r)] = ("sbuf", [128, NP], "uint16")
+        SCRATCH["sm%d%d" % (_c, _r)] = ("sbuf", [128, 8, NB], "bfloat16")
+        SCRATCH["la%d%d" % (_c, _r)] = ("sbuf", [128, NP], "uint16")
+        SCRATCH["lm%d%d" % (_c, _r)] = ("sbuf", [128, 8, NB], "bfloat16")
+        SCRATCH["xo%d%d" % (_c, _r)] = ("sbuf", [128, NP], "uint16")
+        SCRATCH["cp%d%d" % (_c, _r)] = ("sbuf", [128, 8, NB], "bfloat16")
+        SCRATCH["at%d%d" % (_c, _r)] = ("sbuf", [128, 8, NB], "bfloat16")
+SEMAPHORES = ["v", "s", "p", "g", "sent", "lsd", "lact", "lx", "o0", "o1", "o2", "o3"] + \
+             ["arr%d%d" % (c, r) for c in CH for r in RS]
+
+
+def build(g, T, send, narr):
+    ops = []
+    last_w, readers = {}, {}
+
+    def op(eng, calls, R, W, cost, banks=(), sig=None, lat="no"):
+        deps = set()
+        for k in list(R) + list(W):
+            if k in last_w:
+                deps.add(last_w[k])
+        for k in W:
+            deps.update(readers.get(k, ()))
+        i = len(ops)
+        for k in R:
+            readers.setdefault(k, []).append(i)
+        for k in W:
+            last_w[k] = i
+            readers[k] = []
+        deps.discard(i)
+        ops.append(dict(eng=eng, calls=calls, deps=deps, c=cost, banks=tuple(banks), sig=sig, lat=lat, nm=(list(W) + ["-"])[0]))
+
+    V, S, P = g.vector, g.scalar, g.tensor
+
+    def vc(n, f=1.0, k=1):
+        return (0.0, k * max(64.0, n * f), 0, 0)
+
+    def ts(out, in0, s1, s2, o0, o1, R, W, n, banks=()):
+        if o1 is None:
+            op("v", [lambda: V.tensor_scalar(out, in0, s1, None, o0)], R, W, vc(n), banks)
+        else:
+            op("v", [lambda: V.tensor_scalar(out, in0, s1, s2, o0, o1)], R, W, vc(n), banks)
+
+    def tt(out, a, b, o, R, W, n, banks=(), f=None):
+        op("v", [lambda: V.tensor_tensor(out, a, b, o)], R, W, vc(n, f or (1.0 if banks else 2.0)), banks)
+
+    def cp(out, a, R, W, n, banks=()):
+        op("v", [lambda: V.tensor_copy(out, a)], R, W, vc(n), banks)
+
+    def ms(ap, val, W, n):
+        op("v", [lambda: V.memset(ap, val)], [], W, vc(n, 0.5))
+
+    def act(out, a, fn, bias, scale, R, W, n, banks=()):
+        op("s", [lambda: S.activation(out, a, fn, bias=bias, scale=scale)], R, W, vc(n), banks)
+
+    def mm(lst, R, W, banks):
+        calls = [(lambda m=m: P.matmul(m[0], m[1], m[2], m[3], m[4])) for m in lst]
+        op("p", calls, R, W, (0.0, 0, 0, sum(m[5] for m in lst)), banks)
+
+    win = T.xs[:, 0:4112]
+    XW = ["x", "xpad"]
+
+    op("y", [lambda: g.sync.dma_start(T.sdi[:], T.sd[:])], [], ["sd"], (0.1, 0, 0, 0), sig=("lsd", 16), lat="sd")
+    op("y", [lambda: g.sync.dma_start(T.acti[:], T.act[:])], [], ["act"], (0.1, 0, 0, 0), sig=("lact", 16), lat="sd")
+    op("y", [lambda: g.sync.dma_start(T.xs[:, 0:4096], T.x[:])], [], ["x"], (0.1, 0, 0, 0), sig=("lx", 16), lat="x")
+    ms(T.ones[:], 1.0, ["ones"], 128)
+    ms(T.zeros[:], 0.0, ["zeros"], 128)
+    ms(T.xs[:, 4096:4112], 1e29, ["xpad"], 16)
+    op("g", [lambda: g.affine_select(T.eye[:], T.ones[:], [[-1, 128]], A.is_equal, 0.0, 0, 1)], ["ones"], ["eye"], (0.17, 256, 0, 0))
+    op("g", [lambda: g.affine_select(T.grp0[:], T.ones[:, 0:8], [[-16, 8]], A.is_ge, 0.0, 0, 1)], ["ones"], ["grp0"], (0.2, 0, 0, 0))
+    op("g", [lambda: g.affine_select(T.grp[:], T.grp0[:], [[16, 8]], A.is_ge, 0.0, 15, -1)], ["grp0"], ["grp"], (0.2, 0, 0, 0))
+    op("g", [lambda: g.iota(T.qio[:], [[1, 8], [0, NB]], 0, 0, allow_small_or_imprecise_dtypes=True)], [], ["qio"], (0.13, 128, 0, 0))
+    for nm in sorted(EYES):
+        act(T[nm][:], T.eye[:], AF.Copy, 0.0, EYES[nm], ["eye"], [nm], 128)
+    act(T.eyef[:], T.eye[:], AF.Copy, 0.0, 1.0, ["eye"], ["eyef"], 128)
+    tt(T.seye[:], T.eye[:, 0:64], T.eye[:, 64:128], A.add, ["eye"], ["seye"], 64)
+    for c in CH:
+        ms(T["cmp%d" % c][:, 7 * WID:8 * WID], 0.0, ["cmp%d_7_0" % c, "cmp%d_7_1" % c], WID)
+        ms(T["dead%d" % c][:, 2 * NP:3 * NP], 0.0, ["dz%d" % c], NP)
+    op("v", [(lambda q=q: V.tensor_scalar(T.wp[:, 8 + q:64:32, :], T.acti[:], float(q), None, A.is_equal)) for q in range(8)],
+       ["act"], ["L0", "L1"], vc(16, k=8), ["wp"])
+    for k in sorted({n % 4 for n in CFG["ST"].values()} - {0}):
+        op("v", [(lambda u=u, k=k: V.memset(T.tb[32 * u:32 * u + 32, k:k + 1], 1.0 if u < k else -7.5)) for u in range(4)],
+           [], ["tb%d" % k], vc(1, k=4))
+    dtile = [0]
+
+    def lift(c, r):
+        b = slice(c * NB, (c + 1) * NB)
+        cr = "%d%d" % (c, r)
+        src = T.sdi if r == 1 else T.st
+        M = T.wp[:, 32 * c + 8:32 * c + 16, :]
+        pr = T["prod%d" % c]
+        sk = ["sd"] if r == 1 else ["st%d_%d" % (c, k) for k in range(3)]
+        op("v", [(lambda s=s: V.tensor_tensor(pr[:, s:64:8, :], src[:, 8 * s:8 * s + 8, b], M, A.mult)) for s in range(8)],
+           sk + ["L%d" % c], ["prod%d" % c], vc(NP, k=8), ["wp"])
+        sm = T["sm" + cr]
+        ts(sm[:], M, -8 * B, 8 * B, A.mult, A.add, ["L%d" % c], ["sm" + cr], NP, ["wp"])
+        q0 = 32 * c + 16
+        lst = [(T.wp[:, q0:q0 + 16, :], T.eye[:], T.zeros[:], True, False, 128)]
+        for p in range(8):
+            lst.append((T.wp[:, q0 + p + 1:q0 + p + 9, :], T.eyef[:], pr[:, 8 * p:8 * p + 8, :], False, p == 7, 256))
+        mm(lst, ["eye", "zeros", "eyef", "prod%d" % c], ["Q%d" % c], ["wp"])
+        tmp = T["tmp%d" % c]
+        cp(tmp[:], T.wp[:, q0 + 8:q0 + 16, :], ["Q%d" % c], ["tmp%d" % c], NP, ["wp"])
+        tt(tmp[:], T.wp[:, q0:q0 + 8, :], tmp[:], A.add, ["Q%d" % c], ["tmp%d" % c], NP, ["wp"])
+        cp(T["sa" + cr][:], tmp[:], ["tmp%d" % c], ["sa" + cr], NP)
+        op("g", [lambda: send(c, r)], ["sa" + cr, "sm" + cr], ["arr" + cr], (0.3, 0, 0, 0), sig=("arr" + cr, narr), lat="remote")
+        cq = T["cp" + cr]
+        tt(cq[:], T.wp[:, 32 * c:32 * c + 8, :], sm[:], A.min, ["W%d" % c, "sm" + cr], ["cp" + cr], NP, ["wp"])
+        if CFG["SM"][r] == "s":
+            act(T["e8%d" % c][:], cq[:], AF.Relu, -224.0, 32 / B, ["cp" + cr], ["e8%d" % c], NP)
+        else:
+            ts(T["e8%d" % c][:], cq[:], 8 * B, 32.0, A.is_equal, A.mult, ["cp" + cr], ["e8%d" % c], NP)
+
+    for c in CH:
+        b = slice(c * NB, (c + 1) * NB)
+        cp(T["off%d" % c][:], T.sdi[:, :, b], ["sd"], ["off%d" % c], 8 * NP)
+        ts(T.fill[:, c, :], T["off%d" % c][:], F, None, A.is_lt, None, ["off%d" % c], ["fill%d" % c], 4 * NP)
+        mm([(T.wp[:, 32 * c:32 * c + 8, :], T.eyeb[:], T.fill[:, c, NP * s:NP * (s + 1)], s == 0, s == 7, 64) for s in range(8)],
+           ["eyeb", "fill%d" % c], ["W%d" % c], ["wp"])
+        lift(c, 1)
+
+    def gather(eng, out, off, R, W, n):
+        if eng == "s":
+            op("s", [lambda: S.activation(out, win.indirect(off), AF.Copy)], XW + R, W, (0.065, 0, n, 0))
+        else:
+            op("v", [lambda: V.tensor_copy(out, win.indirect(off))], XW + R, W, (0.05, 0, n, 0))
+
+    def rnd(c, r):
+        b = slice(c * NB, (c + 1) * NB)
+        cr = "%d%d" % (c, r)
+        arr = "arr" + cr
+        la, lm, fa = T["la" + cr], T["lm" + cr], T["fa" + cr]
+        fs, cm, thr = T["fs%d" % c], T["cmp%d" % c], T["thr%d" % c]
+        here, af, t = T["here%d" % c], T.vp[:, 32 + 8 * c:40 + 8 * c, :], T["t%d" % c]
+        cq, at, sm = T["cp" + cr], T["at" + cr], T["sm" + cr]
+        dead = T["dead%d" % c]
+        src = T.sdi if r == 1 else T.st
+        for h in (0, 1):
+            gather("s", fa[:, h * 512:(h + 1) * 512], la[:, h * 32:(h + 1) * 32], [arr], ["fa%s_%d" % (cr, h)], 512)
+        if r == 1:
+            for s in range(6):
+                gather("v" if (c, s) in CFG["GV"] else "s", fs[:, s * WID:(s + 1) * WID], T["off%d" % c][:, s * NP:(s + 1) * NP],
+                       ["off%d" % c], ["fs%d_%d" % (c, s)], WID)
+        ts(here[:], la[:], F, None, A.is_lt, None, [arr], ["here%d" % c], NP)
+        cp(af, la[:], [arr], ["af%d" % c], NP, ["vp"])
+        tt(t[:], cq[:], af, A.add, ["cp" + cr, "af%d" % c], ["t%d" % c], NP, ["vp"])
+        op("s", [(lambda s=s: S.activation(T.gp[:, 8 * s:8 * s + 8, :], t[:], AF.Abs, bias=-B * s)) for s in range(1, 8)],
+           ["t%d" % c], ["G"], vc(NP, k=7), ["gp"])
+        tt(T.st[:, 8:64, b], src[:, 8:64, b], T.gp[:, 8:64, :], A.min, ["G", "sd"], ["st%d_1" % c, "st%d_2" % c], 7 * NP, ["gp"])
+        l0 = 32 * c + 8
+        Lp = T.wp[:, l0:l0 + 8, :]
+        mm([(Lp, T.eye[:], here[:], True, False, 64),
+            (T.wp[:, l0:l0 + 7, :], T.neye[:], here[:, 1:8, :], False, False, 64),
+            (T.wp[:, l0 + 7:l0 + 8, :], T.neye[:], here[:, 0:1, :], False, False, 64),
+            (Lp, T.neyem[:], lm[:], False, False, 64),
+            (Lp, T.eye[:], T.ones[:, 0:NP], False, True, 64)],
+           ["eye", "neye", "neyem", "ones", "here%d" % c, arr], ["L%d" % c], ["wp"])
+        ns = CFG["ST"][(c, r)]
+        xo = T["off%d" % c][:, 6 * NP:7 * NP] if r == 1 else T["xo" + cr][:]
+        xk = "off%d" % c if r == 1 else "xo" + cr
+        xs = (c, r) in CFG["XS"]
+        if xs:
+            gather("s", T["xf%d" % c][:], xo, [xk], ["xf%d" % c], WID)
+        else:
+            op("v", [lambda: V.tensor_tensor(cm[:, 6 * WID:7 * WID], win.indirect(xo), fa[:], A.is_lt)],
+               XW + [xk, "fa%s_0" % cr, "fa%s_1" % cr], ["cmp%d_6_0" % c, "cmp%d_6_1" % c], (0.05, 0, WID, 0))
+        for h in (0, 1):
+            fp = T["fa%dp" % h]
+            mm([(fp[:], T.eye[:], fa[:, h * 512:(h + 1) * 512], True, True, 512)], ["eye", "fa%s_%d" % (cr, h)], ["fap%d" % h], ["fa%dp" % h])
+        for h in (0, 1):
+            fp = T["fa%dp" % h]
+            for s in [s for s in range(6) if 2 * s + h >= ns]:
+                o = s * WID + h * 512
+                tt(cm[:, o:o + 512], fs[:, o:o + 512], fp[:], A.is_lt, ["fs%d_%d" % (c, s), "fap%d" % h],
+                   ["cmp%d_%d_%d" % (c, s, h)], 512, ["fa%dp" % h])
+            if xs:
+                o = 6 * WID + h * 512
+                tt(cm[:, o:o + 512], T["xf%d" % c][:, h * 512:(h + 1) * 512], fp[:], A.is_lt, ["xf%d" % c, "fap%d" % h],
+                   ["cmp%d_6_%d" % (c, h)], 512, ["fa%dp" % h])
+            if r == 3:
+                o = 7 * WID + h * 512
+                tt(cm[:, o:o + 512], T["fa%d1" % c][:, h * 512:(h + 1) * 512], fp[:], A.is_lt, ["fa%d1_%d" % (c, h), "fap%d" % h],
+                   ["cmp%d_7_%d" % (c, h)], 512, ["fa%dp" % h])
+        for h in (0, 1):
+            for s in [s for s in range(6) if 2 * s + h < ns]:
+                o = s * WID + h * 512
+                d = dtile[0] % 2
+                dtile[0] += 1
+                dp = T["d%dp" % d]
+                mm([(dp[:], T.eye[:], fa[:, h * 512:(h + 1) * 512], True, False, 512),
+                    (dp[:], T.neye[:], fs[:, o:o + 512], False, True, 512)],
+                   ["eye", "neye", "fa%s_%d" % (cr, h), "fs%d_%d" % (c, s)], ["dp%d" % d], ["d%dp" % d])
+                act(cm[:, o:o + 512], dp[:], AF.Sign, -2.0 ** -70, 1.0, ["dp%d" % d], ["cmp%d_%d_%d" % (c, s, h)], 512, ["d%dp" % d])
+        for pr in (3, 2, 1, 0):
+            lst, R = [], ["grp"]
+            Rp = T.rp[:, pr * 128:(pr + 1) * 128]
+            if r > 1 and pr < 3:
+                lst.append((Rp, dead[:, 0:2 * NP], T.neye[:], True, False, 128))
+                R += ["neye", "dead%d_1" % c]
+                if r == 3:
+                    lst.append((Rp, dead[:, 3 * NP:5 * NP], T.neye[:], False, False, 128))
+                    R += ["dead%d_2" % c]
+            if r == 3 and pr == 3:
+                lst.append((Rp, dead[:, 2 * NP:4 * NP], T.neye[:], True, False, 128))
+                R += ["neye", "dz%d" % c, "dead%d_2" % c]
+            one = not lst
+            for i in range(16):
+                lst.append((T.rp[:, pr * 128 + i:(pr + 1) * 128:16], cm[:, 2 * pr * WID + i:2 * (pr + 1) * WID:16], T.grp[:],
+                            one, one or i == 15, 64))
+            R += ["cmp%d_%d_%d" % (c, s, h) for s in (2 * pr, 2 * pr + 1) for h in (0, 1)]
+            mm(lst, R, ["R%d" % pr], ["rp"])
+            k = min(4, max(0, ns - 4 * pr))
+            act(thr[:, pr * 128:(pr + 1) * 128], Rp, AF.Sign, {0: -7.5, 4: 1.0}[k] if k in (0, 4) else T.tb[:, k:k + 1], 1.0,
+                ["R%d" % pr] + ([] if k in (0, 4) else ["tb%d" % k]), ["thr%d_%d" % (c, pr)], 128, ["rp"])
+        w0 = 32 * c
+        Wp = T.wp[:, w0:w0 + 8, :]
+        lst = [(Wp, T.neyeib[:], cq[:], True, False, 64), (Wp, T.eye[:], T["e8%d" % c][:], False, False, 64),
+               (Wp, T.eyek[:], sm[:], False, False, 64), (Wp, T.eye64[:], here[:], False, False, 64)]
+        lst += [(Wp, thr[:, pr * 128:(pr + 1) * 128], T.seye[:], False, pr == 3, 64) for pr in range(4)]
+        mm(lst, ["neyeib", "eye", "eyek", "eye64", "seye", "cp" + cr, "e8%d" % c, "sm" + cr, "here%d" % c] +
+           ["thr%d_%d" % (c, pr) for pr in range(4)], ["W%d" % c], ["wp"])
+        ncap, y = T["ncap%d" % c], T["y%d" % c]
+        ts(ncap[:], Wp, 120.5, None, A.is_lt, None, ["W%d" % c], ["ncap%d" % c], NP, ["wp"])
+        tt(y[:], Lp, ncap[:], A.mult, ["L%d" % c, "ncap%d" % c], ["y%d" % c], NP, ["wp"])
+        mm([(Lp, T.eye[:], here[:, ::-1, :], True, False, 64),
+            (T.wp[:, l0 + 1:l0 + 8, :], T.neye[:], here[:, 7:0:-1, :], False, False, 64),
+            (T.wp[:, l0:l0 + 1, :], T.neye[:], here[:, 0:1, :], False, False, 64),
+            (Lp, T.neyem[:], lm[:, ::-1, :], False, False, 64),
+            (Lp, T.eye[:], T.ones[:, 0:NP], False, False, 64),
+            (Lp, T.eye[:], y[:], False, False, 64),
+            (Lp, T.neye[:], y[:, ::-1, :], False, True, 64)],
+           ["eye", "neye", "neyem", "ones", "here%d" % c, arr, "y%d" % c], ["L%d" % c], ["wp"])
+        tt(at[:], ncap[:], cq[:], A.mult, ["ncap%d" % c, "cp" + cr], ["at" + cr], NP)
+        clr, m0 = T.vp[:, 16 * c:16 * c + 8, :], T.vp[:, 16 * c + 8:16 * c + 16, :]
+        ts(clr, at[:], 0.0, F, A.is_equal, A.mult, ["at" + cr], ["clr%d" % c], NP, ["vp"])
+        tt(m0, at[:], af, A.max, ["at" + cr, "af%d" % c], ["m%d" % c], NP, ["vp"])
+        tt(T.st[:, 0:8, b], src[:, 0:8, b], clr, A.max, ["sd", "clr%d" % c], ["st%d_0" % c], NP, ["vp"])
+        for k, rows in ((1, range(1, 4)), (2, range(4, 8))):
+            op("v", [(lambda s=s: V.tensor_tensor(T.st[:, 8 * s:8 * s + 8, b], T.st[:, 8 * s:8 * s + 8, b], clr, A.max))
+                     for s in rows], ["clr%d" % c], ["st%d_%d" % (c, k)], vc(NP, k=len(rows)), ["vp"])
+        tt(T.st[:, 0:8, b], T.st[:, 0:8, b], m0, A.min, ["m%d" % c], ["st%d_0" % c], NP, ["vp"])
+        if r < 3:
+            mm([(Wp, T.eye[:], at[:], True, False, 64), (Wp, T.eyeb[:], here[:], False, True, 64)],
+               ["eye", "eyeb", "at" + cr, "here%d" % c], ["W%d" % c], ["wp"])
+            d0 = 0 if r == 1 else 3
+            if CFG["SM"][r] == "s":
+                op("s", [(lambda u=u: S.activation(dead[:, u * NP:(u + 1) * NP], at[:], AF.Relu, bias=F, scale=-1.0)) for u in (d0, d0 + 1)],
+                   ["at" + cr], ["dead%d_%d" % (c, r)], vc(NP, k=2))
+            else:
+                op("v", [(lambda u=u: V.tensor_scalar(dead[:, u * NP:(u + 1) * NP], at[:], 0.0, F, A.is_equal, A.mult)) for u in (d0, d0 + 1)],
+                   ["at" + cr], ["dead%d_%d" % (c, r)], vc(NP, k=2))
+            xk, s6 = T["xk%d" % c], T["s6%d" % c]
+            tt(s6[:], T.sdi[:, 48:56, b] if r == 1 else s6[:], clr, A.max, ["sd", "clr%d" % c], ["s6%d" % c], NP, ["vp"])
+            tt(xk[:], af, s6[:], A.min, ["af%d" % c, "s6%d" % c], ["xk%d" % c], NP, ["vp"])
+            cp(T["xo%d%d" % (c, r + 1)][:], xk[:], ["xk%d" % c], ["xo%d%d" % (c, r + 1)], NP)
+            lift(c, r + 1)
+        else:
+            fin = T["fin%d" % c]
+            lst = []
+            for k in RS:
+                lst.append((Wp, T.eyeib[:], T["cp%d%d" % (c, k)][:], k == 1, False, 64))
+                lst.append((Wp, T.neyeib[:], T["at%d%d" % (c, k)][:], False, k == 3, 64))
+            mm(lst, ["eyeib", "neyeib"] + ["cp%d%d" % (c, k) for k in RS] + ["at%d%d" % (c, k) for k in RS], ["W%d" % c], ["wp"])
+            cp(fin[:, 0, :, :], Wp, ["W%d" % c], ["f0%d" % c], NP, ["wp"])
+            tt(fin[:, 1, :, :], Lp, T.qio[:], A.mult, ["L%d" % c, "qio"], ["f1%d" % c], NP, ["wp"])
+            fk = ["f0%d" % c, "f1%d" % c]
+            tt(fin[:, :, 0:4, :], fin[:, :, 0:4, :], fin[:, :, 4:8, :], A.add, [], fk, 64)
+            tt(fin[:, :, 0:2, :], fin[:, :, 0:2, :], fin[:, :, 2:4, :], A.add, [], fk, 32)
+            tt(T.outp[:, :, b], fin[:, :, 0, :], fin[:, :, 1, :], A.add, fk, ["out%d" % c], 16)
+
+    for r in RS:
+        for c in CH:
+            rnd(c, r)
+    op("y", [lambda: g.sync.dma_start(T.ys[:, 512:1024], T.st[:, 32:64, :])], ["st0_2", "st1_2"], [], (0.1, 0, 0, 0), sig=("o1", 16), lat="out")
+    op("y", [lambda: g.sync.dma_start(T.ys[:, 0:512], T.st[:, 0:32, :])], ["st0_0", "st1_0", "st0_1", "st1_1"], [], (0.1, 0, 0, 0),
+       sig=("o0", 16), lat="out")
+    op("s", [lambda: g.scalar.dma_start(T.yc[:], T.outp[:, 0, :])], ["out0", "out1"], [], (0.1, 0, 0, 0), sig=("o2", 16), lat="small")
+    op("s", [lambda: g.scalar.dma_start(T.yp[:], T.outp[:, 1, :])], ["out0", "out1"], [], (0.1, 0, 0, 0), sig=("o3", 16), lat="small")
+    return ops
+
+
+def halves(topo, src, dst):
+    e = topo.engines(src, dst)[:8]
+    k = len(e) // 2
+    return sum(1 << x for x in e[:k]), sum(1 << x for x in e[k:2 * k]), 2 * k
+
+
+def rank_program(g, core, T, topo):
+    rank = T.rank_of(core)
+    if rank is None:
+        return
+    cores = list(T.cores)
+    nxt, prv = cores[(rank + 1) % len(cores)], cores[(rank - 1) % len(cores)]
+    m0, m1, nsent = halves(topo, core, nxt)
+    narr = halves(topo, prv, core)[2]
+    rid, pid, _ = topo.addr(nxt)
+
+    def send(c, r):
+        sem = T.sem["arr%d%d" % (c, r)]
+        to = [DstId(rid=rid, pnc=pid)]
+        return g.remote_dma_fused([
+            RemoteDMATransfer(dst_ids=to, dma_engine_mask=m0, remote_sem=sem, src=T["sa%d%d" % (c, r)][:], dst=T["la%d%d" % (c, r)][:]),
+            RemoteDMATransfer(dst_ids=to, dma_engine_mask=m1, remote_sem=sem, src=T["sm%d%d" % (c, r)][:], dst=T["lm%d%d" % (c, r)][:]),
+        ], local_sem=T.sem.sent)
+
+    ops = build(g, T, send, narr)
+    order = [0, 1, 2] + [i for i in ORDER if i > 2]
+    assert sorted(order) == list(range(len(ops)))
+    queue = {"v": g.vector, "s": g.scalar, "p": g.tensor, "g": g, "y": g.sync}
+    count = {e: 0 for e in "vspg"}
+    seen = {e: {} for e in queue}
+    bank = {}
+    for i in order:
+        o = ops[i]
+        e = o["eng"]
+        waits = set(o["deps"])
+        for b in o["banks"]:
+            waits.update(d for k, d in bank.get(b, {}).items() if k != e)
+            bank.setdefault(b, {})[e] = i
+        need = {}
+        for d in waits:
+            sem, val = ops[d]["sig"]
+            need[sem] = max(need.get(sem, 0), val)
+        for sem in sorted(need):
+            if seen[e].get(sem, 0) < need[sem]:
+                queue[e].wait_ge(T.sem[sem], need[sem])
+                seen[e][sem] = need[sem]
+        if o["sig"] is None:
+            for call in o["calls"]:
+                call().then_inc(T.sem[e], 1)
+                count[e] += 1
+            o["sig"] = (e, count[e])
+        elif o["sig"][0].startswith("arr"):
+            o["calls"][0]()
+        else:
+            o["calls"][0]().then_inc(T.sem[o["sig"][0]], 16)
+    g.wait_ge(T.sem.sent, nsent * len(CH) * len(RS))
+    for e in "vspg":
+        g.wait_ge(T.sem[e], count[e])
+    for k in range(4):
+        g.sync.wait_ge(T.sem["o%d" % k], 16)

@@ -1,3 +1,5 @@
+import math
+import numpy as np
 from concourse.bass import DstId, RemoteDMATransfer
 from concourse.mybir import AluOpType as A, ActivationFunctionType as AF
 
@@ -6,15 +8,26 @@ B = 8192.0
 NB = 8
 NP = 8 * NB
 WID = 16 * NP
+HALF = WID // 2
 CH = (0, 1)
 RS = (1, 2, 3)
 CFG = {
-    "ST": {(0, 1): 2, (1, 1): 2, (0, 2): 6, (1, 2): 6, (0, 3): 6, (1, 3): 6},
-    "GV": {(0, 1), (0, 2), (1, 1)},
-    "SM": {1: "v", 2: "v", 3: "v"},
-    "XS": {(0, 2), (1, 2), (0, 3), (1, 3)},
+    "WAY": {(0, 1): "dddvvvv", (1, 1): "dddvvvv", (0, 2): "dDDvvvvh", (1, 2): "dDDvvvvh", (0, 3): "ddDDvvvsv", (1, 3): "dDDsvvvvv"},
+    "COPY": 0.85, "ADD": 1.25, "DMA": 1.6, "JOIN": {(0, 1, 1), (0, 2, 1), (1, 1, 2)}, "FOLD": 0.9, "BACK": 3.2, "HELP": 2,
+    "FS": {0: [(e, s, 1) for s, e in enumerate("ssvvvvs")], 1: [(e, s, 1) for s, e in enumerate("sssssvs")]},
+    "FA": {(c, r): "ss" for c in CH for r in RS},
+    "ROWS": [(7,), (6, 5), (4, 3), (2, 1, 0)],
+    "ONS": {"cp2", "cp3", "dead1", "dead2", "e82", "e83", "fin", "last2", "last3", "out", "sm3", "sm2"},
+    "GOALS": ["arr01", "arr11", "arr02", "arr12", "arr03", "arr13", "out0"],
+    "SEQ": [(c, r) for r in RS for c in CH],
+    "TRIES": 30000, "HEAT": 0.08, "COLD": 0.02, "EVEN": 0.3, "ISSUE": 0.8,
+    "CUT": 2, "PASSES": 3, "SEED": 0, "MORE": 2.0, "EARLY": (1, -100), "SFIX": 0.065,
+    "GAT": 1.5, "PE": 0.42e-3, "HOP": 0.1, "REMOTE": 1.5, "SD": 3.0, "X": 5.2,
 }
-ORDER = [22,24,21,2,1,3,6,20,0,19,4,18,23,10,28,17,30,25,37,5,26,38,11,31,29,32,33,41,40,14,27,52,53,13,15,42,16,55,51,34,39,58,35,49,50,43,64,44,36,45,57,54,65,46,78,47,59,69,63,72,68,73,9,67,62,121,74,71,76,7,8,122,56,70,113,114,77,79,84,80,126,75,66,116,81,85,82,115,60,86,87,83,129,61,128,130,88,140,89,123,92,90,91,93,94,95,97,96,98,105,104,117,118,127,132,106,144,107,119,120,108,109,131,110,142,145,141,143,136,137,148,149,124,99,138,135,133,134,139,125,48,101,150,102,103,178,146,187,179,177,186,147,151,100,111,152,196,185,153,156,154,157,155,184,197,158,198,199,160,159,161,162,168,165,166,180,170,167,181,195,191,249,200,171,169,172,201,202,112,173,208,190,189,163,204,194,193,203,175,206,209,182,210,174,192,205,188,207,214,241,212,164,243,215,244,248,260,183,211,213,176,12,216,217,261,220,218,221,222,223,225,226,224,242,250,262,219,264,232,229,245,246,251,234,255,230,254,231,263,266,235,236,233,237,265,268,227,267,252,253,259,256,269,238,270,271,305,278,272,276,258,257,274,247,239,279,307,312,228,308,275,277,273,326,280,306,281,284,282,309,328,285,315,291,283,292,287,286,327,289,288,290,293,297,329,313,314,330,332,331,333,296,294,298,322,321,318,310,299,295,334,335,300,336,344,303,301,316,323,319,320,317,337,324,371,325,342,311,340,302,338,363,364,365,372,384,240,377,386,385,373,388,376,343,387,389,341,375,374,380,390,345,339,381,392,383,346,366,391,347,393,382,378,348,398,402,399,403,350,351,379,367,355,394,357,396,395,353,352,356,304,368,354,358,369,400,370,349,397,401,404,405,359,408,406,409,410,413,411,412,414,360,415,407,417,416,418,361,419,362,420,423,421,422,424]
+POOL = ("d0p", "d1p")
+BANKS = ("fa0p", "fa1p", "mp", "wp", "gp", "vp")
+PLAN = []
+CYC = 0.83e-3
 
 SCRATCH = {
     "xs": ("sbuf", [128, 4112], "bfloat16"),
@@ -23,58 +36,59 @@ SCRATCH = {
     "st": ("sbuf", [128, 64, 16], "float32"),
     "fill": ("sbuf", [128, 2, 8 * NP], "bfloat16"),
     "ones": ("sbuf", [128, 128], "bfloat16"),
-    "zeros": ("sbuf", [128, 128], "bfloat16"),
     "eye": ("sbuf", [128, 128], "bfloat16"),
     "eyef": ("sbuf", [128, 128], "float32"),
     "seye": ("sbuf", [128, NP], "bfloat16"),
     "grp0": ("sbuf", [128, 8], "bfloat16"),
     "grp": ("sbuf", [128, 8], "bfloat16"),
     "qio": ("sbuf", [128, 8, NB], "float32"),
-    "tb": ("sbuf", [128, 4], "float32"),
+    "tb": ("sbuf", [128, 16], "float32"),
+    "base": ("sbuf", [128, 2, 16], "float32"),
     "outp": ("sbuf", [128, 2, 16], "float32"),
     "fa0p": ("psum", [128, 512], "float32"),
     "fa1p": ("psum", [128, 512], "float32"),
     "d0p": ("psum", [128, 512], "float32"),
     "d1p": ("psum", [128, 512], "float32"),
-    "rp": ("psum", [128, 512], "float32"),
+    "mp": ("psum", [128, 64, NB], "float32"),
     "wp": ("psum", [128, 64, NB], "float32"),
     "gp": ("psum", [128, 64, NB], "float32"),
     "vp": ("psum", [128, 64, NB], "float32"),
 }
-EYES = {"neye": -1.0, "eyeb": B, "eyeib": 1 / B, "neyeib": -1 / B, "eye64": 64.0, "eyek": 1 / 1024.0, "neyem": -1 / (8 * B)}
+EYES = {"neye": -1.0, "eyeb": B, "eyeib": 1 / B, "neyeib": -1 / B, "eye64": 64.0, "eye128": 128.0, "neye8b": -8 * B, "eye34": 0.75}
 for _n in EYES:
     SCRATCH[_n] = ("sbuf", [128, 128], "bfloat16")
 for _c in CH:
     SCRATCH["off%d" % _c] = ("sbuf", [128, 8 * NP], "uint16")
-    SCRATCH["fs%d" % _c] = ("sbuf", [128, 6 * WID], "bfloat16")
-    SCRATCH["cmp%d" % _c] = ("sbuf", [128, 8 * WID], "bfloat16")
-    SCRATCH["xf%d" % _c] = ("sbuf", [128, WID], "bfloat16")
-    SCRATCH["thr%d" % _c] = ("sbuf", [128, 512], "bfloat16")
-    SCRATCH["prod%d" % _c] = ("sbuf", [128, 64, NB], "float32")
-    SCRATCH["dead%d" % _c] = ("sbuf", [128, 5 * NP], "bfloat16")
-    SCRATCH["fin%d" % _c] = ("sbuf", [128, 2, 8, NB], "float32")
-    for _n in ("here", "e8", "ncap", "y"):
+    SCRATCH["fs%d" % _c] = ("sbuf", [128, 7 * WID], "bfloat16")
+    SCRATCH["cmp%d" % _c] = ("sbuf", [128, 9 * WID], "bfloat16")
+    SCRATCH["thr%d" % _c] = ("sbuf", [128, 640], "bfloat16")
+    SCRATCH["prod%d" % _c] = ("sbuf", [128, 72, NB], "float32")
+    SCRATCH["dead%d" % _c] = ("sbuf", [128, 6 * NP], "bfloat16")
+    SCRATCH["fin%d" % _c] = ("sbuf", [128, 2, 8, NB], "bfloat16")
+    SCRATCH["t%d" % _c] = ("sbuf", [128, 8, NB], "float32")
+    for _n in ("here", "e8", "last", "y", "pre"):
         SCRATCH["%s%d" % (_n, _c)] = ("sbuf", [128, 8, NB], "bfloat16")
-    for _n in ("t", "tmp", "xk", "s6"):
-        SCRATCH["%s%d" % (_n, _c)] = ("sbuf", [128, 8, NB], "float32")
     for _r in RS:
         SCRATCH["fa%d%d" % (_c, _r)] = ("sbuf", [128, WID], "bfloat16")
         SCRATCH["sa%d%d" % (_c, _r)] = ("sbuf", [128, NP], "uint16")
         SCRATCH["sm%d%d" % (_c, _r)] = ("sbuf", [128, 8, NB], "bfloat16")
         SCRATCH["la%d%d" % (_c, _r)] = ("sbuf", [128, NP], "uint16")
         SCRATCH["lm%d%d" % (_c, _r)] = ("sbuf", [128, 8, NB], "bfloat16")
-        SCRATCH["xo%d%d" % (_c, _r)] = ("sbuf", [128, NP], "uint16")
         SCRATCH["cp%d%d" % (_c, _r)] = ("sbuf", [128, 8, NB], "bfloat16")
-        SCRATCH["at%d%d" % (_c, _r)] = ("sbuf", [128, 8, NB], "bfloat16")
+        if _r < 3:
+            SCRATCH["at%d%d" % (_c, _r)] = ("sbuf", [128, 8, NB], "bfloat16")
 SEMAPHORES = ["v", "s", "p", "g", "sent", "lsd", "lact", "lx", "o0", "o1", "o2", "o3"] + \
-             ["arr%d%d" % (c, r) for c in CH for r in RS]
+             ["%s%d%d" % (k, c, r) for k in ("arr", "mask") for c in CH for r in RS] + \
+             ["%s%d%d%d" % (k, c, r, s) for k in ("cy", "ad") for c in CH for r in RS for s in range(7) if k != "cy" or r < 3]
 
 
-def build(g, T, send, narr):
+def build(g, T, send, narr, fold, nfold):
     ops = []
     last_w, readers = {}, {}
 
-    def op(eng, calls, R, W, cost, banks=(), sig=None, lat="no"):
+    def op(eng, calls, R, W, dur, banks=(), sig=None, lat=0.0, tile=0, more=0.0, res=None, late=((), 0, 0.0)):
+        tardy = {last_w[k] for k in late[0]} - {last_w[k] for k in list(R) + list(W) if k in last_w}
+        R = list(R) + list(late[0])
         deps = set()
         for k in list(R) + list(W):
             if k in last_w:
@@ -88,12 +102,13 @@ def build(g, T, send, narr):
             last_w[k] = i
             readers[k] = []
         deps.discard(i)
-        ops.append(dict(eng=eng, calls=calls, deps=deps, c=cost, banks=tuple(banks), sig=sig, lat=lat, nm=(list(W) + ["-"])[0]))
+        ops.append(dict(eng=eng, calls=calls, deps=deps, dur=dur, banks=tuple(banks), sig=sig, lat=lat, tile=tile, more=more,
+                        res=res or eng, tardy=tardy, head=late[1:], nm=(list(W) + ["-"])[0]))
 
-    V, S, P = g.vector, g.scalar, g.tensor
+    V, S, P = (g.vector, g.scalar, g.tensor) if g is not None else (None, None, None)
 
-    def vc(n, f=1.0, k=1):
-        return (0.0, k * max(64.0, n * f), 0, 0)
+    def vc(n, k=1):
+        return k * max(64.0, n) * CYC
 
     def ts(out, in0, s1, s2, o0, o1, R, W, n, banks=()):
         if o1 is None:
@@ -101,90 +116,106 @@ def build(g, T, send, narr):
         else:
             op("v", [lambda: V.tensor_scalar(out, in0, s1, s2, o0, o1)], R, W, vc(n), banks)
 
-    def tt(out, a, b, o, R, W, n, banks=(), f=None):
-        op("v", [lambda: V.tensor_tensor(out, a, b, o)], R, W, vc(n, f or (1.0 if banks else 2.0)), banks)
+    def tt(out, a, b, o, R, W, n, banks=()):
+        op("v", [lambda: V.tensor_tensor(out, a, b, o)], R, W, vc(n), banks)
 
     def cp(out, a, R, W, n, banks=()):
         op("v", [lambda: V.tensor_copy(out, a)], R, W, vc(n), banks)
 
     def ms(ap, val, W, n):
-        op("v", [lambda: V.memset(ap, val)], [], W, vc(n, 0.5))
+        op("v", [lambda: V.memset(ap, val)], [], W, vc(n))
+
+    def sc(n, k=1):
+        return k * CFG["SFIX"] + vc(n, k)
 
     def act(out, a, fn, bias, scale, R, W, n, banks=()):
-        op("s", [lambda: S.activation(out, a, fn, bias=bias, scale=scale)], R, W, vc(n), banks)
+        op("s", [lambda: S.activation(out, a, fn, bias=bias, scale=scale)], R, W, sc(n), banks)
 
-    def mm(lst, R, W, banks):
+    def either(first, v, s, R, W, banks=()):
+        op(first, *{"v": v, "s": s}[first][:1], R, W, {"v": v, "s": s}[first][1], banks)
+        ops[-1]["alt"] = {"v": v, "s": s}
+
+    def small(name, vcalls, scalls, R, W, banks=()):
+        either("s" if name in CFG["ONS"] else "v", (vcalls, vc(NP, len(vcalls))), (scalls, sc(NP, len(scalls))), R, W, banks)
+
+    def copy(name, out, a, R, W, n, banks):
+        small(name, [lambda: V.tensor_copy(out, a)], [lambda: S.activation(out, a, AF.Copy)], R, W, banks)
+
+    def mm(lst, R, W, banks, more=0.0, late=(), n=0):
         calls = [(lambda m=m: P.matmul(m[0], m[1], m[2], m[3], m[4])) for m in lst]
-        op("p", calls, R, W, (0.0, 0, 0, sum(m[5] for m in lst)), banks)
+        op("p", calls, R, W, sum(m[5] for m in lst) * CFG["PE"], banks, more=more, late=(late, n, sum(m[5] for m in lst[:n]) * CFG["PE"]))
+
+    def signs(lst, R, rows, n, out, bias, R2, W, late=(), k=0):
+        key = "tile%d" % len(ops)
+        op("p", [(lambda bk, m=m: P.matmul(bk[0:rows, m[0]], m[1], m[2], m[3], m[4])) for m in lst], R, [key],
+           sum(m[5] for m in lst) * CFG["PE"], tile=1, late=(late, k, sum(m[5] for m in lst[:k]) * CFG["PE"]))
+        op("s", [lambda bk: S.activation(out, bk[0:rows, 0:n], AF.Sign, bias=bias)], [key] + R2, W, sc(n), tile=2)
 
     win = T.xs[:, 0:4112]
     XW = ["x", "xpad"]
 
-    op("y", [lambda: g.sync.dma_start(T.sdi[:], T.sd[:])], [], ["sd"], (0.1, 0, 0, 0), sig=("lsd", 16), lat="sd")
-    op("y", [lambda: g.sync.dma_start(T.acti[:], T.act[:])], [], ["act"], (0.1, 0, 0, 0), sig=("lact", 16), lat="sd")
-    op("y", [lambda: g.sync.dma_start(T.xs[:, 0:4096], T.x[:])], [], ["x"], (0.1, 0, 0, 0), sig=("lx", 16), lat="x")
-    ms(T.ones[:], 1.0, ["ones"], 128)
-    ms(T.zeros[:], 0.0, ["zeros"], 128)
+    op("y", [lambda: g.sync.dma_start(T.sdi[:], T.sd[:])], [], ["sd"], 0.05, sig=("lsd", 16), lat=CFG["SD"])
+    op("s", [lambda: g.scalar.dma_start(T.acti[:], T.act[:])], [], ["act"], 0.05, sig=("lact", 16), lat=2.0)
+    op("y", [lambda: g.sync.dma_start(T.xs[:, 0:4096], T.x[:])], [], ["x"], 0.05, sig=("lx", 16), lat=CFG["X"])
+    ms(T.ones[:], 1.0, ["ones"], 64)
     ms(T.xs[:, 4096:4112], 1e29, ["xpad"], 16)
-    op("g", [lambda: g.affine_select(T.eye[:], T.ones[:], [[-1, 128]], A.is_equal, 0.0, 0, 1)], ["ones"], ["eye"], (0.17, 256, 0, 0))
-    op("g", [lambda: g.affine_select(T.grp0[:], T.ones[:, 0:8], [[-16, 8]], A.is_ge, 0.0, 0, 1)], ["ones"], ["grp0"], (0.2, 0, 0, 0))
-    op("g", [lambda: g.affine_select(T.grp[:], T.grp0[:], [[16, 8]], A.is_ge, 0.0, 15, -1)], ["grp0"], ["grp"], (0.2, 0, 0, 0))
-    op("g", [lambda: g.iota(T.qio[:], [[1, 8], [0, NB]], 0, 0, allow_small_or_imprecise_dtypes=True)], [], ["qio"], (0.13, 128, 0, 0))
+    ms(T.base[:], 0.0, ["base"], 32)
+    op("g", [lambda: g.affine_select(T.eye[:], T.ones[:], [[-1, 128]], A.is_equal, 0.0, 0, 1)], ["ones"], ["eye"], 0.4)
+    op("g", [lambda: g.affine_select(T.grp0[:], T.ones[:, 0:8], [[-16, 8]], A.is_ge, 0.0, 0, 1)], ["ones"], ["grp0"], 0.2)
+    op("g", [lambda: g.affine_select(T.grp[:], T.grp0[:], [[16, 8]], A.is_ge, 0.0, 15, -1)], ["grp0"], ["grp"], 0.2)
+    op("g", [lambda: g.iota(T.qio[:], [[-int(B), 8], [0, NB]], 0, 0, allow_small_or_imprecise_dtypes=True)], [], ["qio"], 0.25)
     for nm in sorted(EYES):
         act(T[nm][:], T.eye[:], AF.Copy, 0.0, EYES[nm], ["eye"], [nm], 128)
     act(T.eyef[:], T.eye[:], AF.Copy, 0.0, 1.0, ["eye"], ["eyef"], 128)
-    tt(T.seye[:], T.eye[:, 0:64], T.eye[:, 64:128], A.add, ["eye"], ["seye"], 64)
+    tt(T.seye[:], T.eye[:, 0:64], T.eye[:, 64:128], A.add, ["eye"], ["seye"], 128)
     for c in CH:
-        ms(T["cmp%d" % c][:, 7 * WID:8 * WID], 0.0, ["cmp%d_7_0" % c, "cmp%d_7_1" % c], WID)
         ms(T["dead%d" % c][:, 2 * NP:3 * NP], 0.0, ["dz%d" % c], NP)
-    op("v", [(lambda q=q: V.tensor_scalar(T.wp[:, 8 + q:64:32, :], T.acti[:], float(q), None, A.is_equal)) for q in range(8)],
-       ["act"], ["L0", "L1"], vc(16, k=8), ["wp"])
-    for k in sorted({n % 4 for n in CFG["ST"].values()} - {0}):
-        op("v", [(lambda u=u, k=k: V.memset(T.tb[32 * u:32 * u + 32, k:k + 1], 1.0 if u < k else -7.5)) for u in range(4)],
-           [], ["tb%d" % k], vc(1, k=4))
-    dtile = [0]
+        ms(T["prod%d" % c][:, 0:72:9, :], 0.0, ["pz%d" % c], NP)
+    op("v", [(lambda q=q: V.tensor_scalar(T.mp[:, q:16:8, :], T.acti[:], float(q), None, A.is_equal)) for q in range(8)],
+       ["act"], ["L0", "L1"], vc(16, 8), ["mp"])
 
-    def lift(c, r):
+    def bias(k):
+        if "tb%d" % k not in last_w:
+            op("v", [(lambda u=u: V.memset(T.tb[32 * u:32 * u + 32, k:k + 1], 0.5 if k >> u & 1 else -7.5)) for u in range(4)],
+               [], ["tb%d" % k], vc(1, 4))
+        return "tb%d" % k
+
+    Q = T.gp[:, 0:8, :]
+
+    def lift(c, r, cnt, cntR):
         b = slice(c * NB, (c + 1) * NB)
         cr = "%d%d" % (c, r)
         src = T.sdi if r == 1 else T.st
-        M = T.wp[:, 32 * c + 8:32 * c + 16, :]
-        pr = T["prod%d" % c]
-        sk = ["sd"] if r == 1 else ["st%d_%d" % (c, k) for k in range(3)]
-        op("v", [(lambda s=s: V.tensor_tensor(pr[:, s:64:8, :], src[:, 8 * s:8 * s + 8, b], M, A.mult)) for s in range(8)],
-           sk + ["L%d" % c], ["prod%d" % c], vc(NP, k=8), ["wp"])
-        sm = T["sm" + cr]
-        ts(sm[:], M, -8 * B, 8 * B, A.mult, A.add, ["L%d" % c], ["sm" + cr], NP, ["wp"])
-        q0 = 32 * c + 16
-        lst = [(T.wp[:, q0:q0 + 16, :], T.eye[:], T.zeros[:], True, False, 128)]
-        for p in range(8):
-            lst.append((T.wp[:, q0 + p + 1:q0 + p + 9, :], T.eyef[:], pr[:, 8 * p:8 * p + 8, :], False, p == 7, 256))
-        mm(lst, ["eye", "zeros", "eyef", "prod%d" % c], ["Q%d" % c], ["wp"])
-        tmp = T["tmp%d" % c]
-        cp(tmp[:], T.wp[:, q0 + 8:q0 + 16, :], ["Q%d" % c], ["tmp%d" % c], NP, ["wp"])
-        tt(tmp[:], T.wp[:, q0:q0 + 8, :], tmp[:], A.add, ["Q%d" % c], ["tmp%d" % c], NP, ["wp"])
-        cp(T["sa" + cr][:], tmp[:], ["tmp%d" % c], ["sa" + cr], NP)
-        op("g", [lambda: send(c, r)], ["sa" + cr, "sm" + cr], ["arr" + cr], (0.3, 0, 0, 0), sig=("arr" + cr, narr), lat="remote")
-        cq = T["cp" + cr]
-        tt(cq[:], T.wp[:, 32 * c:32 * c + 8, :], sm[:], A.min, ["W%d" % c, "sm" + cr], ["cp" + cr], NP, ["wp"])
-        if CFG["SM"][r] == "s":
-            act(T["e8%d" % c][:], cq[:], AF.Relu, -224.0, 32 / B, ["cp" + cr], ["e8%d" % c], NP)
-        else:
-            ts(T["e8%d" % c][:], cq[:], 8 * B, 32.0, A.is_equal, A.mult, ["cp" + cr], ["e8%d" % c], NP)
+        M = T.mp[:, 8 * c:8 * c + 8, :]
+        pr, sm = T["prod%d" % c], T["sm" + cr]
+        copy("sm%d" % r, sm[:], M, ["L%d" % c], ["sm" + cr], NP, ["mp"])
+        op("g", [lambda: send("m", c, r)], ["sm" + cr], ["mask" + cr], 0.3, sig=("mask" + cr, narr), lat=CFG["REMOTE"])
+        for k, rows in enumerate(CFG["ROWS"]):
+            wins = [s + 1 for s in rows] + [0] * (0 in rows)
+            op("v", [(lambda s=s: V.tensor_tensor(pr[:, 9 * s + 1:9 * s + 9, :], src[:, 8 * s:8 * s + 8, b], M, A.mult)) for s in rows],
+               (["sd"] if r == 1 else ["st%d_%d" % (c, s) for s in rows]) + ["L%d" % c], ["prod%d_%d" % (c, k)], vc(NP, len(rows)), ["mp"])
+            mm([(Q, T.eyef[:], pr[:, 8 * w:8 * w + 8, :], w == 8, w == 0, 256) for w in wins],
+               ["eyef", "pz%d" % c] + ["prod%d_%d" % (c, j) for j in range(k + 1)], ["Q"], ["gp"])
+        cp(T["sa" + cr][:], Q, ["Q"], ["sa" + cr], NP, ["gp"])
+        op("g", [lambda: send("a", c, r)], ["sa" + cr], ["arr" + cr], 0.3, sig=("arr" + cr, narr), lat=CFG["REMOTE"])
+        U = T.wp[:, 32 * c + 16:32 * c + 24, :]
+        mm([(U, l, x, i == 0, False, 64) for i, (l, x) in enumerate(cnt)] + [(U, T.neye8b[:], sm[:], False, True, 64)],
+           cntR + ["neye8b", "sm" + cr], ["U%d" % c], ["wp"])
+        cq, e8 = T["cp" + cr][:], T["e8%d" % c][:]
+        small("cp%d" % r, [lambda: V.tensor_scalar(cq, U, 0.0, None, A.max)], [lambda: S.activation(cq, U, AF.Relu)],
+              ["U%d" % c], ["cp" + cr], ["wp"])
+        small("e8%d" % r, [lambda: V.tensor_scalar(e8, U, 8 * B, 32.0, A.is_equal, A.mult)],
+              [lambda: S.activation(e8, U, AF.Relu, bias=-224.0, scale=32 / B)], ["U%d" % c], ["e8%d" % c], ["wp"])
 
     for c in CH:
         b = slice(c * NB, (c + 1) * NB)
         cp(T["off%d" % c][:], T.sdi[:, :, b], ["sd"], ["off%d" % c], 8 * NP)
         ts(T.fill[:, c, :], T["off%d" % c][:], F, None, A.is_lt, None, ["off%d" % c], ["fill%d" % c], 4 * NP)
-        mm([(T.wp[:, 32 * c:32 * c + 8, :], T.eyeb[:], T.fill[:, c, NP * s:NP * (s + 1)], s == 0, s == 7, 64) for s in range(8)],
-           ["eyeb", "fill%d" % c], ["W%d" % c], ["wp"])
-        lift(c, 1)
+        lift(c, 1, [(T.eyeb[:], T.fill[:, c, NP * s:NP * (s + 1)]) for s in range(8)], ["eyeb", "fill%d" % c])
 
-    def gather(eng, out, off, R, W, n):
-        if eng == "s":
-            op("s", [lambda: S.activation(out, win.indirect(off), AF.Copy)], XW + R, W, (0.065, 0, n, 0))
-        else:
-            op("v", [lambda: V.tensor_copy(out, win.indirect(off))], XW + R, W, (0.05, 0, n, 0))
+    def gather(eng, out, off, R, W, n, scale=1.0):
+        either(eng, ([lambda: V.tensor_scalar(out, win.indirect(off), scale, None, A.mult)], 0.05 + n * CFG["GAT"] * CYC),
+               ([lambda: S.activation(out, win.indirect(off), AF.Copy, scale=scale)], 0.065 + n * CFG["GAT"] * CYC), XW + R, W)
 
     def rnd(c, r):
         b = slice(c * NB, (c + 1) * NB)
@@ -192,210 +223,493 @@ def build(g, T, send, narr):
         arr = "arr" + cr
         la, lm, fa = T["la" + cr], T["lm" + cr], T["fa" + cr]
         fs, cm, thr = T["fs%d" % c], T["cmp%d" % c], T["thr%d" % c]
-        here, af, t = T["here%d" % c], T.vp[:, 32 + 8 * c:40 + 8 * c, :], T["t%d" % c]
-        cq, at, sm = T["cp" + cr], T["at" + cr], T["sm" + cr]
+        here, t, last, y = T["here%d" % c], T["t%d" % c], T["last%d" % c], T["y%d" % c]
+        af, ncap, clr, m0 = [T.vp[:, 32 * c + 8 * k:32 * c + 8 * k + 8, :] for k in range(4)]
+        cq, sm = T["cp" + cr], T["sm" + cr]
+        at = T["at" + cr][:] if r < 3 else T["fin%d" % c][:, 0, :, :]
         dead = T["dead%d" % c]
         src = T.sdi if r == 1 else T.st
+        stk = ["st%d_%d" % (c, s) for s in range(8)]
         for h in (0, 1):
-            gather("s", fa[:, h * 512:(h + 1) * 512], la[:, h * 32:(h + 1) * 32], [arr], ["fa%s_%d" % (cr, h)], 512)
+            gather(CFG["FA"][(c, r)][h], fa[:, h * HALF:(h + 1) * HALF], la[:, h * 32:(h + 1) * 32], [arr], ["fa%s_%d" % (cr, h)], HALF, -1.0)
         if r == 1:
-            for s in range(6):
-                gather("v" if (c, s) in CFG["GV"] else "s", fs[:, s * WID:(s + 1) * WID], T["off%d" % c][:, s * NP:(s + 1) * NP],
-                       ["off%d" % c], ["fs%d_%d" % (c, s)], WID)
+            for e, s0, n in CFG["FS"][c]:
+                gather(e, fs[:, s0 * WID:(s0 + n) * WID], T["off%d" % c][:, s0 * NP:(s0 + n) * NP],
+                       ["off%d" % c], ["fs%d_%d" % (c, s) for s in range(s0, s0 + n)], n * WID)
         ts(here[:], la[:], F, None, A.is_lt, None, [arr], ["here%d" % c], NP)
         cp(af, la[:], [arr], ["af%d" % c], NP, ["vp"])
         tt(t[:], cq[:], af, A.add, ["cp" + cr, "af%d" % c], ["t%d" % c], NP, ["vp"])
         op("s", [(lambda s=s: S.activation(T.gp[:, 8 * s:8 * s + 8, :], t[:], AF.Abs, bias=-B * s)) for s in range(1, 8)],
-           ["t%d" % c], ["G"], vc(NP, k=7), ["gp"])
-        tt(T.st[:, 8:64, b], src[:, 8:64, b], T.gp[:, 8:64, :], A.min, ["G", "sd"], ["st%d_1" % c, "st%d_2" % c], 7 * NP, ["gp"])
-        l0 = 32 * c + 8
-        Lp = T.wp[:, l0:l0 + 8, :]
+           ["t%d" % c], ["G"], sc(NP, 7), ["gp"])
+        tt(T.st[:, 8:64, b], src[:, 8:64, b], T.gp[:, 8:64, :], A.min, ["G", "sd"], stk[1:], 7 * NP, ["gp"])
+        l0 = 8 * c
+        Lp = T.mp[:, l0:l0 + 8, :]
+        ncol = 6 + r
+        top = 65.0 - ncol
         mm([(Lp, T.eye[:], here[:], True, False, 64),
-            (T.wp[:, l0:l0 + 7, :], T.neye[:], here[:, 1:8, :], False, False, 64),
-            (T.wp[:, l0 + 7:l0 + 8, :], T.neye[:], here[:, 0:1, :], False, False, 64),
-            (Lp, T.neyem[:], lm[:], False, False, 64),
-            (Lp, T.eye[:], T.ones[:, 0:NP], False, True, 64)],
-           ["eye", "neye", "neyem", "ones", "here%d" % c, arr], ["L%d" % c], ["wp"])
-        ns = CFG["ST"][(c, r)]
-        xo = T["off%d" % c][:, 6 * NP:7 * NP] if r == 1 else T["xo" + cr][:]
-        xk = "off%d" % c if r == 1 else "xo" + cr
-        xs = (c, r) in CFG["XS"]
-        if xs:
-            gather("s", T["xf%d" % c][:], xo, [xk], ["xf%d" % c], WID)
-        else:
-            op("v", [lambda: V.tensor_tensor(cm[:, 6 * WID:7 * WID], win.indirect(xo), fa[:], A.is_lt)],
-               XW + [xk, "fa%s_0" % cr, "fa%s_1" % cr], ["cmp%d_6_0" % c, "cmp%d_6_1" % c], (0.05, 0, WID, 0))
+            (T.mp[:, l0:l0 + 7, :], T.neye[:], here[:, 1:8, :], False, False, 64),
+            (T.mp[:, l0 + 7:l0 + 8, :], T.neye[:], here[:, 0:1, :], False, False, 64),
+            (Lp, T.eye34[:], sm[:], False, False, 64), (Lp, T.eye[:], lm[:], False, True, 64)],
+           ["eye", "neye", "eye34", "here%d" % c, "sm" + cr, "mask" + cr], ["L%d" % c], ["mp"])
+        small("last%d" % r, [lambda: V.tensor_scalar(last[:], Lp, 256.0, top - 256.0, A.mult, A.add)],
+              [lambda: S.activation(last[:], Lp, AF.Identity, bias=top - 256.0, scale=256.0)], ["L%d" % c], ["last%d" % c], ["mp"])
+        way = CFG["WAY"][(c, r)]
+        bysign = {(s, h) for s in range(ncol) for h in (0, 1) if way[s] == "s" or (way[s] == "h" and h == 0)}
+        cols = [(s, fs, s * WID, ["fs%d_%d" % (c, s)] * 2) for s in range(7)]
+        cols += [(6 + k, T["fa%d%d" % (c, k)], 0, ["fa%d%d_%d" % (c, k, h) for h in (0, 1)]) for k in range(1, r)]
+
+        cut = CFG["CUT"]
+
+        def half(buf, o, h):
+            return buf[:, o + h * HALF:o + (h + 1) * HALF]
+
+        def col_part(buf, o, u, n):
+            return buf[:, o + u * n:o + (u + 1) * n]
+
+        def cks(s, *hs):
+            return ["cmp%d_%d_%d_%d" % (c, s, h, u) for h in hs for u in range(cut)]
+
+        for s, buf, o, key in cols:
+            if way[s] in "fF":
+                ck = cks(s, 0, 1)
+                col = cm[:, s * WID:(s + 1) * WID]
+                op("g", [lambda s=s, col=col, d=buf[:, o:o + WID]: fold(c, r, s, col, d, fa[:])], ["fa%s_0" % cr, "fa%s_1" % cr] + key[:1], ck,
+                   CFG["FOLD"], sig=("ad%s%d" % (cr, s), nfold), lat=CFG["BACK"], res="d")
+                if way[s] == "F":
+                    act(col, col, AF.Sign, -2.0 ** -70, -1.0, ck, ck, WID)
+                    continue
+                n = WID // cut
+                for u in range(cut):
+                    mine = ck[2 * u:2 * u + 2]
+                    ts(col_part(cm, s * WID, u, n), col_part(cm, s * WID, u, n), 0.0, None, A.is_lt, None, mine, mine, n // 2)
+            if way[s] in "dD":
+                ck = cks(s, 0, 1)
+                col, d, dk = cm[:, s * WID:(s + 1) * WID], buf[:, o:o + WID], key[:1]
+                if r < 3:
+                    op("y", [lambda col=col, d=d: g.sync.dma_start(col, d)], dk, ck, CFG["COPY"], sig=("cy%s%d" % (cr, s), 16),
+                       lat=CFG["DMA"], res="d")
+                    d, dk = col, ck
+                db, do = (cm, s * WID) if r < 3 else (buf, o)
+                op("g", [lambda d=d: g.dma_start(d, fa[:], accum_op=A.add)], ["fa%s_0" % cr, "fa%s_1" % cr], dk, CFG["ADD"],
+                   sig=("ad%s%d" % (cr, s), 16), lat=CFG["DMA"], res="d")
+                for h in (0, 1):
+                    mine, to, fr = cks(s, h), half(cm, s * WID, h), half(db, do, h)
+                    either("s" if way[s] == "D" else "v",
+                           ([lambda to=to, fr=fr: V.tensor_scalar(to, fr, 0.0, 0.5, A.is_lt, A.subtract)], vc(HALF // 2)),
+                           ([lambda to=to, fr=fr: S.activation(to, fr, AF.Sign, bias=-2.0 ** -70, scale=-1.0)], sc(HALF)),
+                           mine if r < 3 else dk, mine)
         for h in (0, 1):
             fp = T["fa%dp" % h]
-            mm([(fp[:], T.eye[:], fa[:, h * 512:(h + 1) * 512], True, True, 512)], ["eye", "fa%s_%d" % (cr, h)], ["fap%d" % h], ["fa%dp" % h])
-        for h in (0, 1):
-            fp = T["fa%dp" % h]
-            for s in [s for s in range(6) if 2 * s + h >= ns]:
-                o = s * WID + h * 512
-                tt(cm[:, o:o + 512], fs[:, o:o + 512], fp[:], A.is_lt, ["fs%d_%d" % (c, s), "fap%d" % h],
-                   ["cmp%d_%d_%d" % (c, s, h)], 512, ["fa%dp" % h])
-            if xs:
-                o = 6 * WID + h * 512
-                tt(cm[:, o:o + 512], T["xf%d" % c][:, h * 512:(h + 1) * 512], fp[:], A.is_lt, ["xf%d" % c, "fap%d" % h],
-                   ["cmp%d_6_%d" % (c, h)], 512, ["fa%dp" % h])
-            if r == 3:
-                o = 7 * WID + h * 512
-                tt(cm[:, o:o + 512], T["fa%d1" % c][:, h * 512:(h + 1) * 512], fp[:], A.is_lt, ["fa%d1_%d" % (c, h), "fap%d" % h],
-                   ["cmp%d_7_%d" % (c, h)], 512, ["fa%dp" % h])
-        for h in (0, 1):
-            for s in [s for s in range(6) if 2 * s + h < ns]:
-                o = s * WID + h * 512
-                d = dtile[0] % 2
-                dtile[0] += 1
-                dp = T["d%dp" % d]
-                mm([(dp[:], T.eye[:], fa[:, h * 512:(h + 1) * 512], True, False, 512),
-                    (dp[:], T.neye[:], fs[:, o:o + 512], False, True, 512)],
-                   ["eye", "neye", "fa%s_%d" % (cr, h), "fs%d_%d" % (c, s)], ["dp%d" % d], ["d%dp" % d])
-                act(cm[:, o:o + 512], dp[:], AF.Sign, -2.0 ** -70, 1.0, ["dp%d" % d], ["cmp%d_%d_%d" % (c, s, h)], 512, ["d%dp" % d])
+            if any(w == "v" or (w == "h" and h == 1) for w in way[:7]):
+                mm([(fp[:], T.neye[:], half(fa, 0, h), True, True, HALF)], ["neye", "fa%s_%d" % (cr, h)], ["fap%d" % h],
+                   ["fa%dp" % h], more=CFG["MORE"])
         for pr in (3, 2, 1, 0):
-            lst, R = [], ["grp"]
-            Rp = T.rp[:, pr * 128:(pr + 1) * 128]
-            if r > 1 and pr < 3:
-                lst.append((Rp, dead[:, 0:2 * NP], T.neye[:], True, False, 128))
-                R += ["neye", "dead%d_1" % c]
-                if r == 3:
-                    lst.append((Rp, dead[:, 3 * NP:5 * NP], T.neye[:], False, False, 128))
-                    R += ["dead%d_2" % c]
-            if r == 3 and pr == 3:
-                lst.append((Rp, dead[:, 2 * NP:4 * NP], T.neye[:], True, False, 128))
-                R += ["neye", "dz%d" % c, "dead%d_2" % c]
-            one = not lst
-            for i in range(16):
-                lst.append((T.rp[:, pr * 128 + i:(pr + 1) * 128:16], cm[:, 2 * pr * WID + i:2 * (pr + 1) * WID:16], T.grp[:],
-                            one, one or i == 15, 64))
-            R += ["cmp%d_%d_%d" % (c, s, h) for s in (2 * pr, 2 * pr + 1) for h in (0, 1)]
-            mm(lst, R, ["R%d" % pr], ["rp"])
-            k = min(4, max(0, ns - 4 * pr))
-            act(thr[:, pr * 128:(pr + 1) * 128], Rp, AF.Sign, {0: -7.5, 4: 1.0}[k] if k in (0, 4) else T.tb[:, k:k + 1], 1.0,
-                ["R%d" % pr] + ([] if k in (0, 4) else ["tb%d" % k]), ["thr%d_%d" % (c, pr)], 128, ["rp"])
+            for h in (0, 1):
+                for s, buf, o, key in cols[:7]:
+                    if s // 2 == pr and way[s] in "vh" and (s, h) not in bysign:
+                        n = HALF // cut
+                        for u in range(cut):
+                            lo = h * HALF + u * n
+                            tt(cm[:, s * WID + lo:s * WID + lo + n], buf[:, o + lo:o + lo + n], T["fa%dp" % h][:, u * n:(u + 1) * n], A.is_lt,
+                               [key[h], "fap%d" % h], cks(s, h)[u:u + 1], n, ["fa%dp" % h])
+        for h in (0, 1):
+            old = [(s, buf, key) for s, buf, o, key in cols[7:] if way[s] in "vh" and (s, h) not in bysign]
+            if old:
+                key = "tile%d" % len(ops)
+                op("p", [lambda bk, h=h: P.matmul(bk[:], T.eye[:], half(fa, 0, h), True, True)], ["eye", "fa%s_%d" % (cr, h)], [key],
+                   HALF * CFG["PE"], tile=1)
+                op("v", [(lambda bk, h=h, s=s, buf=buf: V.tensor_tensor(half(cm, s * WID, h), half(buf, 0, h), bk[:], A.is_gt)) for s, buf, k in old],
+                   [key] + [k[h] for s, buf, k in old], [x for s, buf, k in old for x in cks(s, h)], vc(HALF, len(old)), tile=2)
+        for s, buf, o, key in cols:
+            for h in (0, 1):
+                if (s, h) in bysign:
+                    signs([(slice(0, HALF), T.neye[:], half(fa, 0, h), True, False, HALF),
+                           (slice(0, HALF), (T.eye if s > 6 else T.neye)[:], half(buf, o, h), False, True, HALF)],
+                          ["eye", "neye", "fa%s_%d" % (cr, h), key[h]], 128, HALF,
+                          half(cm, s * WID, h), -2.0 ** -70, [], cks(s, h))
+        pairs = [(pr, min(2, ncol - 2 * pr)) for pr in reversed(range((ncol + 1) // 2))]
+        kind = {pr: sum(1 << u for u in range(2 * wide) if (2 * pr + u // 2, u % 2) in bysign or way[2 * pr + u // 2] in "dDF")
+                for pr, wide in pairs}
+        tiles = []
+        for pr, wide in pairs:
+            if tiles and (c, r, pr) in CFG["JOIN"] and tiles[-1][0][1] == wide and kind[tiles[-1][0][0]] == kind[pr]:
+                tiles[-1].insert(0, (pr, wide))
+            else:
+                tiles.append([(pr, wide)])
+        for tl in tiles:
+            lst, R, late = [], ["grp"], []
+            p0, m, k = tl[0][0], NP * tl[0][1], kind[tl[0][0]]
+            for pr, wide in tl:
+                z = 128 * (pr - p0)
+                gone = r > 1 and pr < 4
+                if gone:
+                    u = 3 * (r - 2) + (pr == 3)
+                    lst.append((slice(z, z + 128), dead[:, u * NP:(u + 2) * NP], T.neye[:], True, False, 128))
+                    R += ["neye", "dz%d" % c, "dead%d_%d" % (c, r - 1)]
+                for i in range(16):
+                    lst.append((slice(z + i, z + 128, 16), cm[:, 2 * pr * WID + i:(2 * pr + wide) * WID:16], T.grp[:],
+                                not gone, not gone or i == 15, 64))
+                late += [x for s in range(2 * pr, 2 * pr + wide) for x in cks(s, 0, 1)]
+            n = 128 * len(tl)
+            signs(lst, R, m, n, thr[0:m, p0 * 128:p0 * 128 + n], {0: -7.5, 15: 0.5}[k] if k in (0, 15) else T.tb[0:m, k:k + 1],
+                  [] if k in (0, 15) else [bias(k)], ["thr%d_%d" % (c, pr) for pr, wide in tl], late, int(r > 1 and p0 < 4))
         w0 = 32 * c
         Wp = T.wp[:, w0:w0 + 8, :]
         lst = [(Wp, T.neyeib[:], cq[:], True, False, 64), (Wp, T.eye[:], T["e8%d" % c][:], False, False, 64),
-               (Wp, T.eyek[:], sm[:], False, False, 64), (Wp, T.eye64[:], here[:], False, False, 64)]
-        lst += [(Wp, thr[:, pr * 128:(pr + 1) * 128], T.seye[:], False, pr == 3, 64) for pr in range(4)]
-        mm(lst, ["neyeib", "eye", "eyek", "eye64", "seye", "cp" + cr, "e8%d" % c, "sm" + cr, "here%d" % c] +
-           ["thr%d_%d" % (c, pr) for pr in range(4)], ["W%d" % c], ["wp"])
-        ncap, y = T["ncap%d" % c], T["y%d" % c]
-        ts(ncap[:], Wp, 120.5, None, A.is_lt, None, ["W%d" % c], ["ncap%d" % c], NP, ["wp"])
-        tt(y[:], Lp, ncap[:], A.mult, ["L%d" % c, "ncap%d" % c], ["y%d" % c], NP, ["wp"])
+               (Wp, T.eye128[:], sm[:], False, False, 64), (Wp, T.eye64[:], here[:], False, False, 64)]
+        lst += [(Wp, thr[0:NP * wide, pr * 128:(pr + 1) * 128], T.seye[0:NP * wide, :], False, pr == 0, 64) for pr, wide in pairs]
+        mm(lst, ["neyeib", "eye", "eye128", "eye64", "seye", "cp" + cr, "e8%d" % c, "sm" + cr, "here%d" % c], ["W%d" % c], ["wp"],
+           late=["thr%d_%d" % (c, pr) for pr, wide in pairs], n=4)
+        tt(y[:], Wp, last[:], A.is_lt, ["last%d" % c, "W%d" % c], ["y%d" % c], NP, ["wp"])
+        ts(clr, Wp, top - 0.5, F, A.is_gt, A.mult, ["W%d" % c], ["clr%d" % c], NP, ["wp", "vp"])
+        ts(ncap, Wp, top - 0.5, None, A.is_lt, None, ["W%d" % c], ["ncap%d" % c], NP, ["wp", "vp"])
         mm([(Lp, T.eye[:], here[:, ::-1, :], True, False, 64),
-            (T.wp[:, l0 + 1:l0 + 8, :], T.neye[:], here[:, 7:0:-1, :], False, False, 64),
-            (T.wp[:, l0:l0 + 1, :], T.neye[:], here[:, 0:1, :], False, False, 64),
-            (Lp, T.neyem[:], lm[:, ::-1, :], False, False, 64),
-            (Lp, T.eye[:], T.ones[:, 0:NP], False, False, 64),
-            (Lp, T.eye[:], y[:], False, False, 64),
-            (Lp, T.neye[:], y[:, ::-1, :], False, True, 64)],
-           ["eye", "neye", "neyem", "ones", "here%d" % c, arr, "y%d" % c], ["L%d" % c], ["wp"])
-        tt(at[:], ncap[:], cq[:], A.mult, ["ncap%d" % c, "cp" + cr], ["at" + cr], NP)
-        clr, m0 = T.vp[:, 16 * c:16 * c + 8, :], T.vp[:, 16 * c + 8:16 * c + 16, :]
-        ts(clr, at[:], 0.0, F, A.is_equal, A.mult, ["at" + cr], ["clr%d" % c], NP, ["vp"])
-        tt(m0, at[:], af, A.max, ["at" + cr, "af%d" % c], ["m%d" % c], NP, ["vp"])
-        tt(T.st[:, 0:8, b], src[:, 0:8, b], clr, A.max, ["sd", "clr%d" % c], ["st%d_0" % c], NP, ["vp"])
-        for k, rows in ((1, range(1, 4)), (2, range(4, 8))):
-            op("v", [(lambda s=s: V.tensor_tensor(T.st[:, 8 * s:8 * s + 8, b], T.st[:, 8 * s:8 * s + 8, b], clr, A.max))
-                     for s in rows], ["clr%d" % c], ["st%d_%d" % (c, k)], vc(NP, k=len(rows)), ["vp"])
-        tt(T.st[:, 0:8, b], T.st[:, 0:8, b], m0, A.min, ["m%d" % c], ["st%d_0" % c], NP, ["vp"])
+            (T.mp[:, l0 + 1:l0 + 8, :], T.neye[:], here[:, 7:0:-1, :], False, False, 64),
+            (T.mp[:, l0:l0 + 1, :], T.neye[:], here[:, 0:1, :], False, False, 64),
+            (Lp, T.eye[:], lm[:, ::-1, :], False, False, 64),
+            (Lp, T.eye[:], y[:], False, False, 64), (Lp, T.neye[:], y[:, ::-1, :], False, True, 64)],
+           ["eye", "neye", "here%d" % c, "mask" + cr], ["L%d" % c], ["mp"], late=["y%d" % c], n=4)
+        tt(at, cq[:], ncap, A.mult, ["ncap%d" % c, "cp" + cr], ["at" + cr], NP, ["vp"])
+        tt(m0, at, af, A.max, ["at" + cr, "af%d" % c], ["m%d" % c], NP, ["vp"])
+        for rows in CFG["ROWS"]:
+            op("v", [(lambda s=s: V.tensor_tensor(T.st[:, 8 * s:8 * s + 8, b], (T.st if s else src)[:, 8 * s:8 * s + 8, b], clr, A.max))
+                     for s in rows], ["sd", "clr%d" % c], [stk[s] for s in rows], vc(NP, len(rows)), ["vp"])
+        tt(T.st[:, 0:8, b], T.st[:, 0:8, b], m0, A.min, ["m%d" % c], [stk[0]], NP, ["vp"])
         if r < 3:
-            mm([(Wp, T.eye[:], at[:], True, False, 64), (Wp, T.eyeb[:], here[:], False, True, 64)],
-               ["eye", "eyeb", "at" + cr, "here%d" % c], ["W%d" % c], ["wp"])
-            d0 = 0 if r == 1 else 3
-            if CFG["SM"][r] == "s":
-                op("s", [(lambda u=u: S.activation(dead[:, u * NP:(u + 1) * NP], at[:], AF.Relu, bias=F, scale=-1.0)) for u in (d0, d0 + 1)],
-                   ["at" + cr], ["dead%d_%d" % (c, r)], vc(NP, k=2))
-            else:
-                op("v", [(lambda u=u: V.tensor_scalar(dead[:, u * NP:(u + 1) * NP], at[:], 0.0, F, A.is_equal, A.mult)) for u in (d0, d0 + 1)],
-                   ["at" + cr], ["dead%d_%d" % (c, r)], vc(NP, k=2))
-            xk, s6 = T["xk%d" % c], T["s6%d" % c]
-            tt(s6[:], T.sdi[:, 48:56, b] if r == 1 else s6[:], clr, A.max, ["sd", "clr%d" % c], ["s6%d" % c], NP, ["vp"])
-            tt(xk[:], af, s6[:], A.min, ["af%d" % c, "s6%d" % c], ["xk%d" % c], NP, ["vp"])
-            cp(T["xo%d%d" % (c, r + 1)][:], xk[:], ["xk%d" % c], ["xo%d%d" % (c, r + 1)], NP)
-            lift(c, r + 1)
+            put = [(0, at), (1, at)]
+            if r == 2:
+                kept = T["pre%d" % c][:]
+                tt(kept, T["at%d1" % c][:], ncap, A.mult, ["at%d1" % c, "ncap%d" % c], ["pre%d" % c], NP, ["vp"])
+                put = [(3, kept), (4, kept), (5, at)]
+            R = ["at" + cr] + ["pre%d" % c] * (r == 2)
+            small("dead%d" % r, [(lambda u=u, a=a: V.tensor_scalar(dead[:, u * NP:(u + 1) * NP], a, 0.0, F, A.is_equal, A.mult)) for u, a in put],
+                  [(lambda u=u, a=a: S.activation(dead[:, u * NP:(u + 1) * NP], a, AF.Relu, bias=F, scale=-1.0)) for u, a in put],
+                  R, ["dead%d_%d" % (c, r)])
+            lift(c, r + 1, [(T.eye[:], at), (T.eyeb[:], here[:])], ["eye", "eyeb", "at" + cr, "here%d" % c])
         else:
-            fin = T["fin%d" % c]
-            lst = []
-            for k in RS:
-                lst.append((Wp, T.eyeib[:], T["cp%d%d" % (c, k)][:], k == 1, False, 64))
-                lst.append((Wp, T.neyeib[:], T["at%d%d" % (c, k)][:], False, k == 3, 64))
-            mm(lst, ["eyeib", "neyeib"] + ["cp%d%d" % (c, k) for k in RS] + ["at%d%d" % (c, k) for k in RS], ["W%d" % c], ["wp"])
-            cp(fin[:, 0, :, :], Wp, ["W%d" % c], ["f0%d" % c], NP, ["wp"])
-            tt(fin[:, 1, :, :], Lp, T.qio[:], A.mult, ["L%d" % c, "qio"], ["f1%d" % c], NP, ["wp"])
-            fk = ["f0%d" % c, "f1%d" % c]
-            tt(fin[:, :, 0:4, :], fin[:, :, 0:4, :], fin[:, :, 4:8, :], A.add, [], fk, 64)
-            tt(fin[:, :, 0:2, :], fin[:, :, 0:2, :], fin[:, :, 2:4, :], A.add, [], fk, 32)
-            tt(T.outp[:, :, b], fin[:, :, 0, :], fin[:, :, 1, :], A.add, fk, ["out%d" % c], 16)
+            fin, pre, U, E = T["fin%d" % c], T["pre%d" % c], T.wp[:, w0 + 16:w0 + 24, :], T.wp[:, w0 + 24:w0 + 26, :]
+            lst = [(U, T.eyeib[:], T["cp%d%d" % (c, k)][:], k == 1, False, 64) for k in RS]
+            lst += [(U, T.neyeib[:], T["at%d%d" % (c, k)][:], False, k == 2, 64) for k in RS[:2]]
+            mm(lst, ["eyeib", "neyeib"] + ["cp%d%d" % (c, k) for k in RS] + ["at%d%d" % (c, k) for k in RS[:2]], ["U%d" % c], ["wp"])
+            copy("fin", pre[:], U, ["U%d" % c], ["pre%d" % c], NP, ["wp"])
+            mm([(T.wp[:, w0 + 24, :], T.eye[:], pre[:, q, :], q == 0, q == 7, 64) for q in range(8)], ["eye", "pre%d" % c], ["E%d" % c], ["wp"])
+            copy("out", T.base[:, 0, b], T.wp[:, w0 + 24, :], ["E%d" % c, "base"], ["base%d" % c], NB, ["wp"])
+            tt(fin[:, 1, :, :], T.qio[:], Lp, A.mult, ["L%d" % c, "qio"], ["f1%d" % c], NP, ["mp"])
+            mm([(E, T.neyeib[:], fin[:, :, q, :], q == 0, q == 7, 64) for q in range(8)], ["neyeib", "at" + cr, "f1%d" % c], ["E%d" % c], ["wp"])
+            tt(T.outp[:, :, b], T.base[:, :, b], E, A.add, ["E%d" % c, "base%d" % c], ["out%d" % c], 16, ["wp"])
 
-    for r in RS:
-        for c in CH:
-            rnd(c, r)
-    op("y", [lambda: g.sync.dma_start(T.ys[:, 512:1024], T.st[:, 32:64, :])], ["st0_2", "st1_2"], [], (0.1, 0, 0, 0), sig=("o1", 16), lat="out")
-    op("y", [lambda: g.sync.dma_start(T.ys[:, 0:512], T.st[:, 0:32, :])], ["st0_0", "st1_0", "st0_1", "st1_1"], [], (0.1, 0, 0, 0),
-       sig=("o0", 16), lat="out")
-    op("s", [lambda: g.scalar.dma_start(T.yc[:], T.outp[:, 0, :])], ["out0", "out1"], [], (0.1, 0, 0, 0), sig=("o2", 16), lat="small")
-    op("s", [lambda: g.scalar.dma_start(T.yp[:], T.outp[:, 1, :])], ["out0", "out1"], [], (0.1, 0, 0, 0), sig=("o3", 16), lat="small")
+    for c, r in CFG["SEQ"]:
+        rnd(c, r)
+    for k, rows in ((1, range(4, 8)), (0, range(0, 4))):
+        lo, hi = rows[0], rows[-1] + 1
+        op("y", [lambda lo=lo, hi=hi: g.sync.dma_start(T.ys[:, 128 * lo:128 * hi], T.st[:, 8 * lo:8 * hi, :])],
+           ["st%d_%d" % (c, s) for c in CH for s in rows], [], 0.05, sig=("o%d" % k, 16), lat=3.0)
+    op("s", [lambda: g.scalar.dma_start(T.yc[:], T.outp[:, 0, :])], ["out0", "out1"], [], 0.05, sig=("o2", 16), lat=2.5)
+    op("s", [lambda: g.scalar.dma_start(T.yp[:], T.outp[:, 1, :])], ["out0", "out1"], [], 0.05, sig=("o3", 16), lat=2.5)
     return ops
 
 
-def halves(topo, src, dst):
-    e = topo.engines(src, dst)[:8]
-    k = len(e) // 2
-    return sum(1 << x for x in e[:k]), sum(1 << x for x in e[k:2 * k]), 2 * k
+def place(ops, before, rank, pre, post, mate):
+    hop = CFG["HOP"]
+    n = len(ops)
+    before = [set(b) for b in before]
+    lead = {}
+    for i, o in enumerate(ops):
+        for d in o["tardy"]:
+            lead[(i, d)] = lead[(d, i)] = o["head"][1]
+    for i, j in mate.items():
+        before[i] |= before[j] - {i}
+    users = [[] for _ in ops]
+    for i in range(n):
+        for d in before[i]:
+            users[d].append(i)
+    left = [len(b) for b in before]
+    ready = [i for i in range(n) if not left[i]]
+    start, done, busy, tile = {}, {}, {}, {}
+
+    def gap(i, t):
+        o = ops[i]
+        taken = [x for x in busy.get(o["res"], ()) if x[1] > t]
+        for b in o["banks"]:
+            taken += [(a - hop, z + hop) for a, z, e in busy.get(b, ()) if z + hop > t and e != o["eng"]]
+        taken.sort()
+        for a, z in taken:
+            if a >= t + o["dur"] - 1e-9:
+                break
+            t = max(t, z)
+        return t
+
+    def put(i, t):
+        o = ops[i]
+        start[i], done[i] = t, t + o["dur"] + post[i]
+        busy.setdefault(o["res"], []).append((t, t + o["dur"]))
+        for b in o["banks"]:
+            busy.setdefault(b, []).append((t, t + o["dur"], o["eng"]))
+        for u in users[i]:
+            left[u] -= 1
+            if not left[u] and u not in start and mate.get(i) != u:
+                ready.append(u)
+
+    while ready:
+        i = min(ready, key=lambda j: (rank[j], j))
+        ready.remove(i)
+        t = gap(i, max([0.0] + [done[d] + hop - lead.get((i, d), 0.0) for d in before[i]]) + pre[i])
+        while i in mate:
+            j = mate[i]
+            t2 = gap(j, t + ops[i]["dur"] + hop)
+            end = t2 + ops[j]["dur"] + hop
+            clash = {b: [z for a, z in busy.get(b, []) if a < end - 1e-9 and z > t + 1e-9] for b in POOL}
+            free = [b for b in POOL if not clash[b]]
+            if free:
+                tile[i] = tile[j] = free[0]
+                busy.setdefault(free[0], []).append((t, end))
+                break
+            t = gap(i, min(min(z) for z in clash.values()))
+        put(i, t)
+        if i in mate:
+            put(j, t2)
+    return start, done, tile
+
+
+def schedule(ops):
+    hop = CFG["HOP"]
+    n = len(ops)
+    deps = [o["deps"] for o in ops]
+    users = [set() for _ in ops]
+    for i in range(n):
+        for d in deps[i]:
+            users[d].add(i)
+    goals = sorted((i for i in range(n) if ops[i]["nm"] in CFG["GOALS"]), key=lambda i: CFG["GOALS"].index(ops[i]["nm"]))
+    way = [None] * n
+    for i in reversed(range(n)):
+        own = ops[i]["dur"] + ops[i]["lat"]
+        if i in goals:
+            way[i] = (goals.index(i), -own)
+        else:
+            k, w = min([way[u] for u in users[i]] + [(len(goals), hop)])
+            way[i] = (k, w - hop - own - ops[i]["more"])
+            if ops[i]["nm"].startswith("fa") and ops[i]["eng"] != "p" or ops[i]["res"] == "d":
+                way[i] = (k - CFG["EARLY"][0], way[i][1] - CFG["EARLY"][1])
+    lat, none = [o["lat"] for o in ops], [0.0] * n
+    mate = {i: i + 1 for i in range(n) if ops[i]["tile"] == 1}
+    start, done, tile = place(ops, deps, way, none, lat, mate)
+    best = (max(done.values()), start)
+    for k in range(CFG["PASSES"]):
+        back = place(ops, users, [-done[i] for i in range(n)], lat, none, {j: i for i, j in mate.items()})[1]
+        start, done, tile = place(ops, deps, [-back[i] for i in range(n)], none, lat, mate)
+        best = min(best, (max(done.values()), start), key=lambda x: x[0])
+    return improve(ops, [0, 1, 2] + sorted(range(3, n), key=lambda i: (best[1][i], i)))
+
+
+def improve(ops, order):
+    hop, n = CFG["HOP"], len(ops)
+    eng = [o["eng"] for o in ops]
+    dur = [o["dur"] for o in ops]
+    need = [[(d, hop - (o["head"][1] if d in o["tardy"] else 0.0)) for d in sorted(o["deps"])] for o in ops]
+    fixed = [(o["lat"], o["banks"], o["tile"], (CFG["ISSUE"] if o["eng"] == "g" else 0.05) if o["res"] == "d" else None) for o in ops]
+    flex = [i for i in range(n) if "alt" in ops[i]]
+
+    def replay(order):
+        done, why = [0.0] * n, [-1] * n
+        free, bank, tile = {e: (0.0, -1) for e in "vspgyd"}, {b: ("", -1, -1) for b in BANKS}, {}
+        pool = {b: (0.0, -1) for b in POOL}
+        for i in order:
+            e = eng[i]
+            lat, banks, half, issue = fixed[i]
+            t, w = free[e]
+            for d, h in need[i]:
+                h += done[d]
+                if h > t:
+                    t, w = h, d
+            for b in banks:
+                k, d, prior = bank[b]
+                if k == e:
+                    d = prior
+                bank[b] = (e, i, d)
+                if d >= 0 and done[d] + hop > t:
+                    t, w = done[d] + hop, d
+            if half == 1:
+                if not pool:
+                    return None
+                b = tile[i] = tile[i + 1] = min(pool, key=pool.get)
+                t, w = max((t, w), pool.pop(b))
+            if issue:
+                free[e] = (t + issue, i)
+                t, w = max((t, w), free["d"])
+                e = "d"
+            why[i] = w
+            t += dur[i]
+            free[e] = (t, i)
+            done[i] = t + lat
+            if half == 2:
+                pool[tile[i]] = (t + hop, i)
+        end = max(done)
+        return end + CFG["EVEN"] * max(load.values()), done.index(end), why, tile, end
+
+    def flip(steps):
+        for i in steps:
+            load[eng[i]] -= dur[i]
+            eng[i] = "s" if eng[i] == "v" else "v"
+            dur[i] = ops[i]["alt"][eng[i]][1]
+            load[eng[i]] += dur[i]
+
+    load = {e: sum(dur[i] for i in range(n) if eng[i] == e) + (2.0 if e == "s" else 0.0) for e in "vs"}
+    cur = replay(order)
+    best = (cur[0], order, cur[3], list(eng), cur[4])
+    rounds = CFG["TRIES"]
+    dice = np.random.RandomState(CFG["SEED"]).rand(rounds, 6).tolist()
+    for k, (a, b, c, d, e, f) in enumerate(dice):
+        slack = -CFG["HEAT"] * (CFG["COLD"] / CFG["HEAT"]) ** (k / rounds) * math.log(1.0 - f)
+        chain, i = [], cur[1]
+        while cur[2][i] >= 0:
+            if cur[2][i] not in ops[i]["deps"]:
+                chain.append((cur[2][i], i))
+            i = cur[2][i]
+        if a < 0.1:
+            near = [x for pair in chain for x in pair if "alt" in ops[x]] if b < 0.7 else []
+            steps = [(near or flex)[int(c * len(near or flex))]]
+            other = flex[int(d * len(flex))]
+            steps += [other] * (e < 0.4 and eng[other] != eng[steps[0]])
+            flip(steps)
+            new, trial = replay(order), order
+            if new[0] > cur[0] + slack:
+                flip(steps)
+                continue
+        else:
+            if chain and b < 0.8:
+                j, i = chain[int(c * len(chain))]
+                lo, hi = order.index(j), order.index(i)
+            else:
+                lo = 3 + int(c * (n - 4))
+                hi = min(n - 1, lo + 1 + int(d * 11))
+            if lo < 3 or lo >= hi:
+                continue
+            part = order[lo:hi + 1]
+            if e < 0.5:
+                move = {part[-1]}
+                for x in reversed(part):
+                    if x in move:
+                        move |= ops[x]["deps"]
+                stay = part[0] in move
+                part = [x for x in part if x in move] + [x for x in part if x not in move]
+            else:
+                move = {part[0]}
+                for x in part:
+                    if ops[x]["deps"] & move:
+                        move.add(x)
+                stay = part[-1] in move
+                part = [x for x in part if x not in move] + [x for x in part if x in move]
+            if stay:
+                continue
+            trial = order[:lo] + part + order[hi + 1:]
+            new = replay(trial)
+            if new is None or new[0] > cur[0] + slack:
+                continue
+        order, cur = trial, new
+        if cur[0] < best[0]:
+            best = (cur[0], order, cur[3], list(eng), cur[4])
+    CFG["EST"] = best[4]
+    return best[1:4]
+
+
+def engines(topo, cores):
+    sets = [set(topo.engines(a, b)) for a, b in zip(cores, cores[1:] + cores[:1])]
+    return sorted(set.intersection(*sets))
+
+
+def helpers(T, topo, core):
+    return [k for k in topo.cores_of(core) if T.rank_of(k) is None and topo.die(k) == topo.die(core)][:CFG["HELP"]]
+
+
+def plan(T, topo):
+    if not PLAN:
+        ops = build(None, T, None, 0, None, 0)
+        order, tile, takes = schedule(ops)
+        names = [ops[i]["sig"][0] for i in order if ops[i]["res"] == "d"]
+        folds = [k for k in names if CFG["WAY"][(int(k[2]), int(k[3]))][int(k[4])] in "fF"]
+        PLAN.extend([order, tile, folds, takes])
+    return PLAN
+
+
+def hand_on(g, core, T, topo):
+    for owner in T.cores:
+        mine = helpers(T, topo, owner)
+        if core in mine:
+            rid, pid, _ = topo.addr(owner)
+            n = len(topo.engines(core, owner))
+            todo = plan(T, topo)[2][mine.index(core)::len(mine)]
+            for name in todo:
+                c, s = int(name[2]), int(name[4])
+                col = T["cmp%d" % c][:, s * WID:(s + 1) * WID]
+                g.wait_ge(T.sem[name], n)
+                g.remote_dma(col, col, T.sem[name], T.sem.sent, pid, rid, topo.mask(core, owner))
+            if todo:
+                g.wait_ge(T.sem.sent, n * len(todo))
 
 
 def rank_program(g, core, T, topo):
     rank = T.rank_of(core)
     if rank is None:
+        hand_on(g, core, T, topo)
         return
     cores = list(T.cores)
-    nxt, prv = cores[(rank + 1) % len(cores)], cores[(rank - 1) % len(cores)]
-    m0, m1, nsent = halves(topo, core, nxt)
-    narr = halves(topo, prv, core)[2]
-    rid, pid, _ = topo.addr(nxt)
+    eng = engines(topo, cores)
+    mask, narr = sum(1 << x for x in eng), len(eng)
+    rid, pid, _ = topo.addr(cores[(rank + 1) % len(cores)])
+    order, tile, folds, takes = plan(T, topo)
+    mine = helpers(T, topo, core)
+    nfold = len(topo.engines(core, mine[0]))
 
-    def send(c, r):
-        sem = T.sem["arr%d%d" % (c, r)]
-        to = [DstId(rid=rid, pnc=pid)]
-        return g.remote_dma_fused([
-            RemoteDMATransfer(dst_ids=to, dma_engine_mask=m0, remote_sem=sem, src=T["sa%d%d" % (c, r)][:], dst=T["la%d%d" % (c, r)][:]),
-            RemoteDMATransfer(dst_ids=to, dma_engine_mask=m1, remote_sem=sem, src=T["sm%d%d" % (c, r)][:], dst=T["lm%d%d" % (c, r)][:]),
-        ], local_sem=T.sem.sent)
+    def send(k, c, r):
+        sem = T.sem["%s%d%d" % ({"a": "arr", "m": "mask"}[k], c, r)]
+        return g.remote_dma(T["l%s%d%d" % (k, c, r)][:], T["s%s%d%d" % (k, c, r)][:], sem, T.sem.sent, pid, rid, mask)
 
-    ops = build(g, T, send, narr)
-    order = [0, 1, 2] + [i for i in ORDER if i > 2]
-    assert sorted(order) == list(range(len(ops)))
+    def fold(c, r, s, col, a, b):
+        name = "ad%d%d%d" % (c, r, s)
+        to = mine[folds.index(name) % len(mine)]
+        hr, hp, _ = topo.addr(to)
+        return g.remote_dma_fused([RemoteDMATransfer(dst_ids=[DstId(rid=hr, pnc=hp)], dma_engine_mask=topo.mask(core, to),
+                                                     remote_sem=T.sem[name], srcs=[a, b], dsts=[col], alu_op=1)], local_sem=T.sem.sent)
+
+    ops = build(g, T, send, narr, fold, nfold)
     queue = {"v": g.vector, "s": g.scalar, "p": g.tensor, "g": g, "y": g.sync}
     count = {e: 0 for e in "vspg"}
     seen = {e: {} for e in queue}
     bank = {}
-    for i in order:
-        o = ops[i]
-        e = o["eng"]
-        waits = set(o["deps"])
-        for b in o["banks"]:
-            waits.update(d for k, d in bank.get(b, {}).items() if k != e)
-            bank.setdefault(b, {})[e] = i
+
+    def wait(e, steps):
         need = {}
-        for d in waits:
+        for d in steps:
             sem, val = ops[d]["sig"]
             need[sem] = max(need.get(sem, 0), val)
         for sem in sorted(need):
             if seen[e].get(sem, 0) < need[sem]:
                 queue[e].wait_ge(T.sem[sem], need[sem])
                 seen[e][sem] = need[sem]
+
+    for i in order:
+        o = ops[i]
+        e = takes[i]
+        if "alt" in o:
+            o["calls"] = o["alt"][e][0]
+        waits = o["deps"] - o["tardy"]
+        args = [T[tile[i]]] if o["tile"] else []
+        for b in o["banks"] + ((tile[i],) if o["tile"] else ()):
+            waits.update(d for k, d in bank.get(b, {}).items() if k != e)
+            bank.setdefault(b, {})[e] = i
+        wait(e, waits)
         if o["sig"] is None:
-            for call in o["calls"]:
-                call().then_inc(T.sem[e], 1)
+            for k, call in enumerate(o["calls"]):
+                if k == o["head"][0]:
+                    wait(e, o["tardy"])
+                call(*args).then_inc(T.sem[e], 1)
                 count[e] += 1
             o["sig"] = (e, count[e])
-        elif o["sig"][0].startswith("arr"):
+        elif o["sig"][0].startswith(("arr", "mask")) or o["sig"][0] in folds:
             o["calls"][0]()
         else:
             o["calls"][0]().then_inc(T.sem[o["sig"][0]], 16)
-    g.wait_ge(T.sem.sent, nsent * len(CH) * len(RS))
+    g.wait_ge(T.sem.sent, narr * 2 * len(CH) * len(RS) + nfold * len(folds))
     for e in "vspg":
         g.wait_ge(T.sem[e], count[e])
     for k in range(4):

import math
import numpy as np
from concourse.bass import DstId, RemoteDMATransfer
from concourse.mybir import AluOpType as A, ActivationFunctionType as AF

F = 4096.0
B = 8192.0
NB = 8
NP = 8 * NB
WID = 16 * NP
HALF = WID // 2
CH = (0, 1)
RS = (1, 2, 3)
CFG = {
    "WAY": {(0, 1): "dddvvvv", (1, 1): "dddvvvv", (0, 2): "dDDvvvvh", (1, 2): "dDDvvvvh", (0, 3): "ddDDvvvsv", (1, 3): "dDDsvvvvv"},
    "COPY": 0.85, "ADD": 1.25, "DMA": 1.6, "JOIN": {(0, 1, 1), (0, 2, 1), (1, 1, 2)}, "FOLD": 0.9, "BACK": 3.2, "HELP": 2,
    "FS": {0: [(e, s, 1) for s, e in enumerate("ssvvvvs")], 1: [(e, s, 1) for s, e in enumerate("sssssvs")]},
    "FA": {(c, r): "ss" for c in CH for r in RS},
    "ROWS": [(7,), (6, 5), (4, 3), (2, 1, 0)],
    "ONS": {"cp2", "cp3", "dead1", "dead2", "e82", "e83", "fin", "last2", "last3", "out", "sm3", "sm2"},
    "GOALS": ["arr01", "arr11", "arr02", "arr12", "arr03", "arr13", "out0"],
    "SEQ": [(c, r) for r in RS for c in CH],
    "TRIES": 30000, "HEAT": 0.08, "COLD": 0.02, "EVEN": 0.3, "ISSUE": 0.8,
    "CUT": 2, "PASSES": 3, "SEED": 0, "MORE": 2.0, "EARLY": (1, -100), "SFIX": 0.065,
    "GAT": 1.5, "PE": 0.42e-3, "HOP": 0.1, "REMOTE": 1.5, "SD": 3.0, "X": 5.2,
}
POOL = ("d0p", "d1p")
BANKS = ("fa0p", "fa1p", "mp", "wp", "gp", "vp")
PLAN = []
CYC = 0.83e-3

SCRATCH = {
    "xs": ("sbuf", [128, 4112], "bfloat16"),
    "sdi": ("sbuf", [128, 64, 16], "int32"),
    "acti": ("sbuf", [128, 2, NB], "int32"),
    "st": ("sbuf", [128, 64, 16], "float32"),
    "fill": ("sbuf", [128, 2, 8 * NP], "bfloat16"),
    "ones": ("sbuf", [128, 128], "bfloat16"),
    "eye": ("sbuf", [128, 128], "bfloat16"),
    "eyef": ("sbuf", [128, 128], "float32"),
    "seye": ("sbuf", [128, NP], "bfloat16"),
    "grp0": ("sbuf", [128, 8], "bfloat16"),
    "grp": ("sbuf", [128, 8], "bfloat16"),
    "qio": ("sbuf", [128, 8, NB], "float32"),
    "tb": ("sbuf", [128, 16], "float32"),
    "base": ("sbuf", [128, 2, 16], "float32"),
    "outp": ("sbuf", [128, 2, 16], "float32"),
    "fa0p": ("psum", [128, 512], "float32"),
    "fa1p": ("psum", [128, 512], "float32"),
    "d0p": ("psum", [128, 512], "float32"),
    "d1p": ("psum", [128, 512], "float32"),
    "mp": ("psum", [128, 64, NB], "float32"),
    "wp": ("psum", [128, 64, NB], "float32"),
    "gp": ("psum", [128, 64, NB], "float32"),
    "vp": ("psum", [128, 64, NB], "float32"),
}
EYES = {"neye": -1.0, "eyeb": B, "eyeib": 1 / B, "neyeib": -1 / B, "eye64": 64.0, "eye128": 128.0, "neye8b": -8 * B, "eye34": 0.75}
for _n in EYES:
    SCRATCH[_n] = ("sbuf", [128, 128], "bfloat16")
for _c in CH:
    SCRATCH["off%d" % _c] = ("sbuf", [128, 8 * NP], "uint16")
    SCRATCH["fs%d" % _c] = ("sbuf", [128, 7 * WID], "bfloat16")
    SCRATCH["cmp%d" % _c] = ("sbuf", [128, 9 * WID], "bfloat16")
    SCRATCH["thr%d" % _c] = ("sbuf", [128, 640], "bfloat16")
    SCRATCH["prod%d" % _c] = ("sbuf", [128, 72, NB], "float32")
    SCRATCH["dead%d" % _c] = ("sbuf", [128, 6 * NP], "bfloat16")
    SCRATCH["fin%d" % _c] = ("sbuf", [128, 2, 8, NB], "bfloat16")
    SCRATCH["t%d" % _c] = ("sbuf", [128, 8, NB], "float32")
    for _n in ("here", "e8", "last", "y", "pre"):
        SCRATCH["%s%d" % (_n, _c)] = ("sbuf", [128, 8, NB], "bfloat16")
    for _r in RS:
        SCRATCH["fa%d%d" % (_c, _r)] = ("sbuf", [128, WID], "bfloat16")
        SCRATCH["sa%d%d" % (_c, _r)] = ("sbuf", [128, NP], "uint16")
        SCRATCH["sm%d%d" % (_c, _r)] = ("sbuf", [128, 8, NB], "bfloat16")
        SCRATCH["la%d%d" % (_c, _r)] = ("sbuf", [128, NP], "uint16")
        SCRATCH["lm%d%d" % (_c, _r)] = ("sbuf", [128, 8, NB], "bfloat16")
        SCRATCH["cp%d%d" % (_c, _r)] = ("sbuf", [128, 8, NB], "bfloat16")
        if _r < 3:
            SCRATCH["at%d%d" % (_c, _r)] = ("sbuf", [128, 8, NB], "bfloat16")
SEMAPHORES = ["v", "s", "p", "g", "sent", "lsd", "lact", "lx", "o0", "o1", "o2", "o3"] + \
             ["%s%d%d" % (k, c, r) for k in ("arr", "mask") for c in CH for r in RS] + \
             ["%s%d%d%d" % (k, c, r, s) for k in ("cy", "ad") for c in CH for r in RS for s in range(7) if k != "cy" or r < 3]


def build(g, T, send, narr, fold, nfold):
    ops = []
    last_w, readers = {}, {}

    def op(eng, calls, R, W, dur, banks=(), sig=None, lat=0.0, tile=0, more=0.0, res=None, late=((), 0, 0.0)):
        tardy = {last_w[k] for k in late[0]} - {last_w[k] for k in list(R) + list(W) if k in last_w}
        R = list(R) + list(late[0])
        deps = set()
        for k in list(R) + list(W):
            if k in last_w:
                deps.add(last_w[k])
        for k in W:
            deps.update(readers.get(k, ()))
        i = len(ops)
        for k in R:
            readers.setdefault(k, []).append(i)
        for k in W:
            last_w[k] = i
            readers[k] = []
        deps.discard(i)
        ops.append(dict(eng=eng, calls=calls, deps=deps, dur=dur, banks=tuple(banks), sig=sig, lat=lat, tile=tile, more=more,
                        res=res or eng, tardy=tardy, head=late[1:], nm=(list(W) + ["-"])[0]))

    V, S, P = (g.vector, g.scalar, g.tensor) if g is not None else (None, None, None)

    def vc(n, k=1):
        return k * max(64.0, n) * CYC

    def ts(out, in0, s1, s2, o0, o1, R, W, n, banks=()):
        if o1 is None:
            op("v", [lambda: V.tensor_scalar(out, in0, s1, None, o0)], R, W, vc(n), banks)
        else:
            op("v", [lambda: V.tensor_scalar(out, in0, s1, s2, o0, o1)], R, W, vc(n), banks)

    def tt(out, a, b, o, R, W, n, banks=()):
        op("v", [lambda: V.tensor_tensor(out, a, b, o)], R, W, vc(n), banks)

    def cp(out, a, R, W, n, banks=()):
        op("v", [lambda: V.tensor_copy(out, a)], R, W, vc(n), banks)

    def ms(ap, val, W, n):
        op("v", [lambda: V.memset(ap, val)], [], W, vc(n))

    def sc(n, k=1):
        return k * CFG["SFIX"] + vc(n, k)

    def act(out, a, fn, bias, scale, R, W, n, banks=()):
        op("s", [lambda: S.activation(out, a, fn, bias=bias, scale=scale)], R, W, sc(n), banks)

    def either(first, v, s, R, W, banks=()):
        op(first, *{"v": v, "s": s}[first][:1], R, W, {"v": v, "s": s}[first][1], banks)
        ops[-1]["alt"] = {"v": v, "s": s}

    def small(name, vcalls, scalls, R, W, banks=()):
        either("s" if name in CFG["ONS"] else "v", (vcalls, vc(NP, len(vcalls))), (scalls, sc(NP, len(scalls))), R, W, banks)

    def copy(name, out, a, R, W, n, banks):
        small(name, [lambda: V.tensor_copy(out, a)], [lambda: S.activation(out, a, AF.Copy)], R, W, banks)

    def mm(lst, R, W, banks, more=0.0, late=(), n=0):
        calls = [(lambda m=m: P.matmul(m[0], m[1], m[2], m[3], m[4])) for m in lst]
        op("p", calls, R, W, sum(m[5] for m in lst) * CFG["PE"], banks, more=more, late=(late, n, sum(m[5] for m in lst[:n]) * CFG["PE"]))

    def signs(lst, R, rows, n, out, bias, R2, W, late=(), k=0):
        key = "tile%d" % len(ops)
        op("p", [(lambda bk, m=m: P.matmul(bk[0:rows, m[0]], m[1], m[2], m[3], m[4])) for m in lst], R, [key],
           sum(m[5] for m in lst) * CFG["PE"], tile=1, late=(late, k, sum(m[5] for m in lst[:k]) * CFG["PE"]))
        op("s", [lambda bk: S.activation(out, bk[0:rows, 0:n], AF.Sign, bias=bias)], [key] + R2, W, sc(n), tile=2)

    win = T.xs[:, 0:4112]
    XW = ["x", "xpad"]

    op("y", [lambda: g.sync.dma_start(T.sdi[:], T.sd[:])], [], ["sd"], 0.05, sig=("lsd", 16), lat=CFG["SD"])
    op("s", [lambda: g.scalar.dma_start(T.acti[:], T.act[:])], [], ["act"], 0.05, sig=("lact", 16), lat=2.0)
    op("y", [lambda: g.sync.dma_start(T.xs[:, 0:4096], T.x[:])], [], ["x"], 0.05, sig=("lx", 16), lat=CFG["X"])
    ms(T.ones[:], 1.0, ["ones"], 64)
    ms(T.xs[:, 4096:4112], 1e29, ["xpad"], 16)
    ms(T.base[:], 0.0, ["base"], 32)
    op("g", [lambda: g.affine_select(T.eye[:], T.ones[:], [[-1, 128]], A.is_equal, 0.0, 0, 1)], ["ones"], ["eye"], 0.4)
    op("g", [lambda: g.affine_select(T.grp0[:], T.ones[:, 0:8], [[-16, 8]], A.is_ge, 0.0, 0, 1)], ["ones"], ["grp0"], 0.2)
    op("g", [lambda: g.affine_select(T.grp[:], T.grp0[:], [[16, 8]], A.is_ge, 0.0, 15, -1)], ["grp0"], ["grp"], 0.2)
    op("g", [lambda: g.iota(T.qio[:], [[-int(B), 8], [0, NB]], 0, 0, allow_small_or_imprecise_dtypes=True)], [], ["qio"], 0.25)
    for nm in sorted(EYES):
        act(T[nm][:], T.eye[:], AF.Copy, 0.0, EYES[nm], ["eye"], [nm], 128)
    act(T.eyef[:], T.eye[:], AF.Copy, 0.0, 1.0, ["eye"], ["eyef"], 128)
    tt(T.seye[:], T.eye[:, 0:64], T.eye[:, 64:128], A.add, ["eye"], ["seye"], 128)
    for c in CH:
        ms(T["dead%d" % c][:, 2 * NP:3 * NP], 0.0, ["dz%d" % c], NP)
        ms(T["prod%d" % c][:, 0:72:9, :], 0.0, ["pz%d" % c], NP)
    op("v", [(lambda q=q: V.tensor_scalar(T.mp[:, q:16:8, :], T.acti[:], float(q), None, A.is_equal)) for q in range(8)],
       ["act"], ["L0", "L1"], vc(16, 8), ["mp"])

    def bias(k):
        if "tb%d" % k not in last_w:
            op("v", [(lambda u=u: V.memset(T.tb[32 * u:32 * u + 32, k:k + 1], 0.5 if k >> u & 1 else -7.5)) for u in range(4)],
               [], ["tb%d" % k], vc(1, 4))
        return "tb%d" % k

    Q = T.gp[:, 0:8, :]

    def lift(c, r, cnt, cntR):
        b = slice(c * NB, (c + 1) * NB)
        cr = "%d%d" % (c, r)
        src = T.sdi if r == 1 else T.st
        M = T.mp[:, 8 * c:8 * c + 8, :]
        pr, sm = T["prod%d" % c], T["sm" + cr]
        copy("sm%d" % r, sm[:], M, ["L%d" % c], ["sm" + cr], NP, ["mp"])
        op("g", [lambda: send("m", c, r)], ["sm" + cr], ["mask" + cr], 0.3, sig=("mask" + cr, narr), lat=CFG["REMOTE"])
        for k, rows in enumerate(CFG["ROWS"]):
            wins = [s + 1 for s in rows] + [0] * (0 in rows)
            op("v", [(lambda s=s: V.tensor_tensor(pr[:, 9 * s + 1:9 * s + 9, :], src[:, 8 * s:8 * s + 8, b], M, A.mult)) for s in rows],
               (["sd"] if r == 1 else ["st%d_%d" % (c, s) for s in rows]) + ["L%d" % c], ["prod%d_%d" % (c, k)], vc(NP, len(rows)), ["mp"])
            mm([(Q, T.eyef[:], pr[:, 8 * w:8 * w + 8, :], w == 8, w == 0, 256) for w in wins],
               ["eyef", "pz%d" % c] + ["prod%d_%d" % (c, j) for j in range(k + 1)], ["Q"], ["gp"])
        cp(T["sa" + cr][:], Q, ["Q"], ["sa" + cr], NP, ["gp"])
        op("g", [lambda: send("a", c, r)], ["sa" + cr], ["arr" + cr], 0.3, sig=("arr" + cr, narr), lat=CFG["REMOTE"])
        U = T.wp[:, 32 * c + 16:32 * c + 24, :]
        mm([(U, l, x, i == 0, False, 64) for i, (l, x) in enumerate(cnt)] + [(U, T.neye8b[:], sm[:], False, True, 64)],
           cntR + ["neye8b", "sm" + cr], ["U%d" % c], ["wp"])
        cq, e8 = T["cp" + cr][:], T["e8%d" % c][:]
        small("cp%d" % r, [lambda: V.tensor_scalar(cq, U, 0.0, None, A.max)], [lambda: S.activation(cq, U, AF.Relu)],
              ["U%d" % c], ["cp" + cr], ["wp"])
        small("e8%d" % r, [lambda: V.tensor_scalar(e8, U, 8 * B, 32.0, A.is_equal, A.mult)],
              [lambda: S.activation(e8, U, AF.Relu, bias=-224.0, scale=32 / B)], ["U%d" % c], ["e8%d" % c], ["wp"])

    for c in CH:
        b = slice(c * NB, (c + 1) * NB)
        cp(T["off%d" % c][:], T.sdi[:, :, b], ["sd"], ["off%d" % c], 8 * NP)
        ts(T.fill[:, c, :], T["off%d" % c][:], F, None, A.is_lt, None, ["off%d" % c], ["fill%d" % c], 4 * NP)
        lift(c, 1, [(T.eyeb[:], T.fill[:, c, NP * s:NP * (s + 1)]) for s in range(8)], ["eyeb", "fill%d" % c])

    def gather(eng, out, off, R, W, n, scale=1.0):
        either(eng, ([lambda: V.tensor_scalar(out, win.indirect(off), scale, None, A.mult)], 0.05 + n * CFG["GAT"] * CYC),
               ([lambda: S.activation(out, win.indirect(off), AF.Copy, scale=scale)], 0.065 + n * CFG["GAT"] * CYC), XW + R, W)

    def rnd(c, r):
        b = slice(c * NB, (c + 1) * NB)
        cr = "%d%d" % (c, r)
        arr = "arr" + cr
        la, lm, fa = T["la" + cr], T["lm" + cr], T["fa" + cr]
        fs, cm, thr = T["fs%d" % c], T["cmp%d" % c], T["thr%d" % c]
        here, t, last, y = T["here%d" % c], T["t%d" % c], T["last%d" % c], T["y%d" % c]
        af, ncap, clr, m0 = [T.vp[:, 32 * c + 8 * k:32 * c + 8 * k + 8, :] for k in range(4)]
        cq, sm = T["cp" + cr], T["sm" + cr]
        at = T["at" + cr][:] if r < 3 else T["fin%d" % c][:, 0, :, :]
        dead = T["dead%d" % c]
        src = T.sdi if r == 1 else T.st
        stk = ["st%d_%d" % (c, s) for s in range(8)]
        for h in (0, 1):
            gather(CFG["FA"][(c, r)][h], fa[:, h * HALF:(h + 1) * HALF], la[:, h * 32:(h + 1) * 32], [arr], ["fa%s_%d" % (cr, h)], HALF, -1.0)
        if r == 1:
            for e, s0, n in CFG["FS"][c]:
                gather(e, fs[:, s0 * WID:(s0 + n) * WID], T["off%d" % c][:, s0 * NP:(s0 + n) * NP],
                       ["off%d" % c], ["fs%d_%d" % (c, s) for s in range(s0, s0 + n)], n * WID)
        ts(here[:], la[:], F, None, A.is_lt, None, [arr], ["here%d" % c], NP)
        cp(af, la[:], [arr], ["af%d" % c], NP, ["vp"])
        tt(t[:], cq[:], af, A.add, ["cp" + cr, "af%d" % c], ["t%d" % c], NP, ["vp"])
        op("s", [(lambda s=s: S.activation(T.gp[:, 8 * s:8 * s + 8, :], t[:], AF.Abs, bias=-B * s)) for s in range(1, 8)],
           ["t%d" % c], ["G"], sc(NP, 7), ["gp"])
        tt(T.st[:, 8:64, b], src[:, 8:64, b], T.gp[:, 8:64, :], A.min, ["G", "sd"], stk[1:], 7 * NP, ["gp"])
        l0 = 8 * c
        Lp = T.mp[:, l0:l0 + 8, :]
        ncol = 6 + r
        top = 65.0 - ncol
        mm([(Lp, T.eye[:], here[:], True, False, 64),
            (T.mp[:, l0:l0 + 7, :], T.neye[:], here[:, 1:8, :], False, False, 64),
            (T.mp[:, l0 + 7:l0 + 8, :], T.neye[:], here[:, 0:1, :], False, False, 64),
            (Lp, T.eye34[:], sm[:], False, False, 64), (Lp, T.eye[:], lm[:], False, True, 64)],
           ["eye", "neye", "eye34", "here%d" % c, "sm" + cr, "mask" + cr], ["L%d" % c], ["mp"])
        small("last%d" % r, [lambda: V.tensor_scalar(last[:], Lp, 256.0, top - 256.0, A.mult, A.add)],
              [lambda: S.activation(last[:], Lp, AF.Identity, bias=top - 256.0, scale=256.0)], ["L%d" % c], ["last%d" % c], ["mp"])
        way = CFG["WAY"][(c, r)]
        bysign = {(s, h) for s in range(ncol) for h in (0, 1) if way[s] == "s" or (way[s] == "h" and h == 0)}
        cols = [(s, fs, s * WID, ["fs%d_%d" % (c, s)] * 2) for s in range(7)]
        cols += [(6 + k, T["fa%d%d" % (c, k)], 0, ["fa%d%d_%d" % (c, k, h) for h in (0, 1)]) for k in range(1, r)]

        cut = CFG["CUT"]

        def half(buf, o, h):
            return buf[:, o + h * HALF:o + (h + 1) * HALF]

        def col_part(buf, o, u, n):
            return buf[:, o + u * n:o + (u + 1) * n]

        def cks(s, *hs):
            return ["cmp%d_%d_%d_%d" % (c, s, h, u) for h in hs for u in range(cut)]

        for s, buf, o, key in cols:
            if way[s] in "fF":
                ck = cks(s, 0, 1)
                col = cm[:, s * WID:(s + 1) * WID]
                op("g", [lambda s=s, col=col, d=buf[:, o:o + WID]: fold(c, r, s, col, d, fa[:])], ["fa%s_0" % cr, "fa%s_1" % cr] + key[:1], ck,
                   CFG["FOLD"], sig=("ad%s%d" % (cr, s), nfold), lat=CFG["BACK"], res="d")
                if way[s] == "F":
                    act(col, col, AF.Sign, -2.0 ** -70, -1.0, ck, ck, WID)
                    continue
                n = WID // cut
                for u in range(cut):
                    mine = ck[2 * u:2 * u + 2]
                    ts(col_part(cm, s * WID, u, n), col_part(cm, s * WID, u, n), 0.0, None, A.is_lt, None, mine, mine, n // 2)
            if way[s] in "dD":
                ck = cks(s, 0, 1)
                col, d, dk = cm[:, s * WID:(s + 1) * WID], buf[:, o:o + WID], key[:1]
                if r < 3:
                    op("y", [lambda col=col, d=d: g.sync.dma_start(col, d)], dk, ck, CFG["COPY"], sig=("cy%s%d" % (cr, s), 16),
                       lat=CFG["DMA"], res="d")
                    d, dk = col, ck
                db, do = (cm, s * WID) if r < 3 else (buf, o)
                op("g", [lambda d=d: g.dma_start(d, fa[:], accum_op=A.add)], ["fa%s_0" % cr, "fa%s_1" % cr], dk, CFG["ADD"],
                   sig=("ad%s%d" % (cr, s), 16), lat=CFG["DMA"], res="d")
                for h in (0, 1):
                    mine, to, fr = cks(s, h), half(cm, s * WID, h), half(db, do, h)
                    either("s" if way[s] == "D" else "v",
                           ([lambda to=to, fr=fr: V.tensor_scalar(to, fr, 0.0, 0.5, A.is_lt, A.subtract)], vc(HALF // 2)),
                           ([lambda to=to, fr=fr: S.activation(to, fr, AF.Sign, bias=-2.0 ** -70, scale=-1.0)], sc(HALF)),
                           mine if r < 3 else dk, mine)
        for h in (0, 1):
            fp = T["fa%dp" % h]
            if any(w == "v" or (w == "h" and h == 1) for w in way[:7]):
                mm([(fp[:], T.neye[:], half(fa, 0, h), True, True, HALF)], ["neye", "fa%s_%d" % (cr, h)], ["fap%d" % h],
                   ["fa%dp" % h], more=CFG["MORE"])
        for pr in (3, 2, 1, 0):
            for h in (0, 1):
                for s, buf, o, key in cols[:7]:
                    if s // 2 == pr and way[s] in "vh" and (s, h) not in bysign:
                        n = HALF // cut
                        for u in range(cut):
                            lo = h * HALF + u * n
                            tt(cm[:, s * WID + lo:s * WID + lo + n], buf[:, o + lo:o + lo + n], T["fa%dp" % h][:, u * n:(u + 1) * n], A.is_lt,
                               [key[h], "fap%d" % h], cks(s, h)[u:u + 1], n, ["fa%dp" % h])
        for h in (0, 1):
            old = [(s, buf, key) for s, buf, o, key in cols[7:] if way[s] in "vh" and (s, h) not in bysign]
            if old:
                key = "tile%d" % len(ops)
                op("p", [lambda bk, h=h: P.matmul(bk[:], T.eye[:], half(fa, 0, h), True, True)], ["eye", "fa%s_%d" % (cr, h)], [key],
                   HALF * CFG["PE"], tile=1)
                op("v", [(lambda bk, h=h, s=s, buf=buf: V.tensor_tensor(half(cm, s * WID, h), half(buf, 0, h), bk[:], A.is_gt)) for s, buf, k in old],
                   [key] + [k[h] for s, buf, k in old], [x for s, buf, k in old for x in cks(s, h)], vc(HALF, len(old)), tile=2)
        for s, buf, o, key in cols:
            for h in (0, 1):
                if (s, h) in bysign:
                    signs([(slice(0, HALF), T.neye[:], half(fa, 0, h), True, False, HALF),
                           (slice(0, HALF), (T.eye if s > 6 else T.neye)[:], half(buf, o, h), False, True, HALF)],
                          ["eye", "neye", "fa%s_%d" % (cr, h), key[h]], 128, HALF,
                          half(cm, s * WID, h), -2.0 ** -70, [], cks(s, h))
        pairs = [(pr, min(2, ncol - 2 * pr)) for pr in reversed(range((ncol + 1) // 2))]
        kind = {pr: sum(1 << u for u in range(2 * wide) if (2 * pr + u // 2, u % 2) in bysign or way[2 * pr + u // 2] in "dDF")
                for pr, wide in pairs}
        tiles = []
        for pr, wide in pairs:
            if tiles and (c, r, pr) in CFG["JOIN"] and tiles[-1][0][1] == wide and kind[tiles[-1][0][0]] == kind[pr]:
                tiles[-1].insert(0, (pr, wide))
            else:
                tiles.append([(pr, wide)])
        for tl in tiles:
            lst, R, late = [], ["grp"], []
            p0, m, k = tl[0][0], NP * tl[0][1], kind[tl[0][0]]
            for pr, wide in tl:
                z = 128 * (pr - p0)
                gone = r > 1 and pr < 4
                if gone:
                    u = 3 * (r - 2) + (pr == 3)
                    lst.append((slice(z, z + 128), dead[:, u * NP:(u + 2) * NP], T.neye[:], True, False, 128))
                    R += ["neye", "dz%d" % c, "dead%d_%d" % (c, r - 1)]
                for i in range(16):
                    lst.append((slice(z + i, z + 128, 16), cm[:, 2 * pr * WID + i:(2 * pr + wide) * WID:16], T.grp[:],
                                not gone, not gone or i == 15, 64))
                late += [x for s in range(2 * pr, 2 * pr + wide) for x in cks(s, 0, 1)]
            n = 128 * len(tl)
            signs(lst, R, m, n, thr[0:m, p0 * 128:p0 * 128 + n], {0: -7.5, 15: 0.5}[k] if k in (0, 15) else T.tb[0:m, k:k + 1],
                  [] if k in (0, 15) else [bias(k)], ["thr%d_%d" % (c, pr) for pr, wide in tl], late, int(r > 1 and p0 < 4))
        w0 = 32 * c
        Wp = T.wp[:, w0:w0 + 8, :]
        lst = [(Wp, T.neyeib[:], cq[:], True, False, 64), (Wp, T.eye[:], T["e8%d" % c][:], False, False, 64),
               (Wp, T.eye128[:], sm[:], False, False, 64), (Wp, T.eye64[:], here[:], False, False, 64)]
        lst += [(Wp, thr[0:NP * wide, pr * 128:(pr + 1) * 128], T.seye[0:NP * wide, :], False, pr == 0, 64) for pr, wide in pairs]
        mm(lst, ["neyeib", "eye", "eye128", "eye64", "seye", "cp" + cr, "e8%d" % c, "sm" + cr, "here%d" % c], ["W%d" % c], ["wp"],
           late=["thr%d_%d" % (c, pr) for pr, wide in pairs], n=4)
        tt(y[:], Wp, last[:], A.is_lt, ["last%d" % c, "W%d" % c], ["y%d" % c], NP, ["wp"])
        ts(clr, Wp, top - 0.5, F, A.is_gt, A.mult, ["W%d" % c], ["clr%d" % c], NP, ["wp", "vp"])
        ts(ncap, Wp, top - 0.5, None, A.is_lt, None, ["W%d" % c], ["ncap%d" % c], NP, ["wp", "vp"])
        mm([(Lp, T.eye[:], here[:, ::-1, :], True, False, 64),
            (T.mp[:, l0 + 1:l0 + 8, :], T.neye[:], here[:, 7:0:-1, :], False, False, 64),
            (T.mp[:, l0:l0 + 1, :], T.neye[:], here[:, 0:1, :], False, False, 64),
            (Lp, T.eye[:], lm[:, ::-1, :], False, False, 64),
            (Lp, T.eye[:], y[:], False, False, 64), (Lp, T.neye[:], y[:, ::-1, :], False, True, 64)],
           ["eye", "neye", "here%d" % c, "mask" + cr], ["L%d" % c], ["mp"], late=["y%d" % c], n=4)
        tt(at, cq[:], ncap, A.mult, ["ncap%d" % c, "cp" + cr], ["at" + cr], NP, ["vp"])
        tt(m0, at, af, A.max, ["at" + cr, "af%d" % c], ["m%d" % c], NP, ["vp"])
        for rows in CFG["ROWS"]:
            op("v", [(lambda s=s: V.tensor_tensor(T.st[:, 8 * s:8 * s + 8, b], (T.st if s else src)[:, 8 * s:8 * s + 8, b], clr, A.max))
                     for s in rows], ["sd", "clr%d" % c], [stk[s] for s in rows], vc(NP, len(rows)), ["vp"])
        tt(T.st[:, 0:8, b], T.st[:, 0:8, b], m0, A.min, ["m%d" % c], [stk[0]], NP, ["vp"])
        if r < 3:
            put = [(0, at), (1, at)]
            if r == 2:
                kept = T["pre%d" % c][:]
                tt(kept, T["at%d1" % c][:], ncap, A.mult, ["at%d1" % c, "ncap%d" % c], ["pre%d" % c], NP, ["vp"])
                put = [(3, kept), (4, kept), (5, at)]
            R = ["at" + cr] + ["pre%d" % c] * (r == 2)
            small("dead%d" % r, [(lambda u=u, a=a: V.tensor_scalar(dead[:, u * NP:(u + 1) * NP], a, 0.0, F, A.is_equal, A.mult)) for u, a in put],
                  [(lambda u=u, a=a: S.activation(dead[:, u * NP:(u + 1) * NP], a, AF.Relu, bias=F, scale=-1.0)) for u, a in put],
                  R, ["dead%d_%d" % (c, r)])
            lift(c, r + 1, [(T.eye[:], at), (T.eyeb[:], here[:])], ["eye", "eyeb", "at" + cr, "here%d" % c])
        else:
            fin, pre, U, E = T["fin%d" % c], T["pre%d" % c], T.wp[:, w0 + 16:w0 + 24, :], T.wp[:, w0 + 24:w0 + 26, :]
            lst = [(U, T.eyeib[:], T["cp%d%d" % (c, k)][:], k == 1, False, 64) for k in RS]
            lst += [(U, T.neyeib[:], T["at%d%d" % (c, k)][:], False, k == 2, 64) for k in RS[:2]]
            mm(lst, ["eyeib", "neyeib"] + ["cp%d%d" % (c, k) for k in RS] + ["at%d%d" % (c, k) for k in RS[:2]], ["U%d" % c], ["wp"])
            copy("fin", pre[:], U, ["U%d" % c], ["pre%d" % c], NP, ["wp"])
            mm([(T.wp[:, w0 + 24, :], T.eye[:], pre[:, q, :], q == 0, q == 7, 64) for q in range(8)], ["eye", "pre%d" % c], ["E%d" % c], ["wp"])
            copy("out", T.base[:, 0, b], T.wp[:, w0 + 24, :], ["E%d" % c, "base"], ["base%d" % c], NB, ["wp"])
            tt(fin[:, 1, :, :], T.qio[:], Lp, A.mult, ["L%d" % c, "qio"], ["f1%d" % c], NP, ["mp"])
            mm([(E, T.neyeib[:], fin[:, :, q, :], q == 0, q == 7, 64) for q in range(8)], ["neyeib", "at" + cr, "f1%d" % c], ["E%d" % c], ["wp"])
            tt(T.outp[:, :, b], T.base[:, :, b], E, A.add, ["E%d" % c, "base%d" % c], ["out%d" % c], 16, ["wp"])

    for c, r in CFG["SEQ"]:
        rnd(c, r)
    for k, rows in ((1, range(4, 8)), (0, range(0, 4))):
        lo, hi = rows[0], rows[-1] + 1
        op("y", [lambda lo=lo, hi=hi: g.sync.dma_start(T.ys[:, 128 * lo:128 * hi], T.st[:, 8 * lo:8 * hi, :])],
           ["st%d_%d" % (c, s) for c in CH for s in rows], [], 0.05, sig=("o%d" % k, 16), lat=3.0)
    op("s", [lambda: g.scalar.dma_start(T.yc[:], T.outp[:, 0, :])], ["out0", "out1"], [], 0.05, sig=("o2", 16), lat=2.5)
    op("s", [lambda: g.scalar.dma_start(T.yp[:], T.outp[:, 1, :])], ["out0", "out1"], [], 0.05, sig=("o3", 16), lat=2.5)
    return ops


def place(ops, before, rank, pre, post, mate):
    hop = CFG["HOP"]
    n = len(ops)
    before = [set(b) for b in before]
    lead = {}
    for i, o in enumerate(ops):
        for d in o["tardy"]:
            lead[(i, d)] = lead[(d, i)] = o["head"][1]
    for i, j in mate.items():
        before[i] |= before[j] - {i}
    users = [[] for _ in ops]
    for i in range(n):
        for d in before[i]:
            users[d].append(i)
    left = [len(b) for b in before]
    ready = [i for i in range(n) if not left[i]]
    start, done, busy, tile = {}, {}, {}, {}

    def gap(i, t):
        o = ops[i]
        taken = [x for x in busy.get(o["res"], ()) if x[1] > t]
        for b in o["banks"]:
            taken += [(a - hop, z + hop) for a, z, e in busy.get(b, ()) if z + hop > t and e != o["eng"]]
        taken.sort()
        for a, z in taken:
            if a >= t + o["dur"] - 1e-9:
                break
            t = max(t, z)
        return t

    def put(i, t):
        o = ops[i]
        start[i], done[i] = t, t + o["dur"] + post[i]
        busy.setdefault(o["res"], []).append((t, t + o["dur"]))
        for b in o["banks"]:
            busy.setdefault(b, []).append((t, t + o["dur"], o["eng"]))
        for u in users[i]:
            left[u] -= 1
            if not left[u] and u not in start and mate.get(i) != u:
                ready.append(u)

    while ready:
        i = min(ready, key=lambda j: (rank[j], j))
        ready.remove(i)
        t = gap(i, max([0.0] + [done[d] + hop - lead.get((i, d), 0.0) for d in before[i]]) + pre[i])
        while i in mate:
            j = mate[i]
            t2 = gap(j, t + ops[i]["dur"] + hop)
            end = t2 + ops[j]["dur"] + hop
            clash = {b: [z for a, z in busy.get(b, []) if a < end - 1e-9 and z > t + 1e-9] for b in POOL}
            free = [b for b in POOL if not clash[b]]
            if free:
                tile[i] = tile[j] = free[0]
                busy.setdefault(free[0], []).append((t, end))
                break
            t = gap(i, min(min(z) for z in clash.values()))
        put(i, t)
        if i in mate:
            put(j, t2)
    return start, done, tile


def schedule(ops):
    hop = CFG["HOP"]
    n = len(ops)
    deps = [o["deps"] for o in ops]
    users = [set() for _ in ops]
    for i in range(n):
        for d in deps[i]:
            users[d].add(i)
    goals = sorted((i for i in range(n) if ops[i]["nm"] in CFG["GOALS"]), key=lambda i: CFG["GOALS"].index(ops[i]["nm"]))
    way = [None] * n
    for i in reversed(range(n)):
        own = ops[i]["dur"] + ops[i]["lat"]
        if i in goals:
            way[i] = (goals.index(i), -own)
        else:
            k, w = min([way[u] for u in users[i]] + [(len(goals), hop)])
            way[i] = (k, w - hop - own - ops[i]["more"])
            if ops[i]["nm"].startswith("fa") and ops[i]["eng"] != "p" or ops[i]["res"] == "d":
                way[i] = (k - CFG["EARLY"][0], way[i][1] - CFG["EARLY"][1])
    lat, none = [o["lat"] for o in ops], [0.0] * n
    mate = {i: i + 1 for i in range(n) if ops[i]["tile"] == 1}
    start, done, tile = place(ops, deps, way, none, lat, mate)
    best = (max(done.values()), start)
    for k in range(CFG["PASSES"]):
        back = place(ops, users, [-done[i] for i in range(n)], lat, none, {j: i for i, j in mate.items()})[1]
        start, done, tile = place(ops, deps, [-back[i] for i in range(n)], none, lat, mate)
        best = min(best, (max(done.values()), start), key=lambda x: x[0])
    return improve(ops, [0, 1, 2] + sorted(range(3, n), key=lambda i: (best[1][i], i)))


def improve(ops, order):
    hop, n = CFG["HOP"], len(ops)
    eng = [o["eng"] for o in ops]
    dur = [o["dur"] for o in ops]
    need = [[(d, hop - (o["head"][1] if d in o["tardy"] else 0.0)) for d in sorted(o["deps"])] for o in ops]
    fixed = [(o["lat"], o["banks"], o["tile"], (CFG["ISSUE"] if o["eng"] == "g" else 0.05) if o["res"] == "d" else None) for o in ops]
    flex = [i for i in range(n) if "alt" in ops[i]]

    def replay(order):
        done, why = [0.0] * n, [-1] * n
        free, bank, tile = {e: (0.0, -1) for e in "vspgyd"}, {b: ("", -1, -1) for b in BANKS}, {}
        pool = {b: (0.0, -1) for b in POOL}
        for i in order:
            e = eng[i]
            lat, banks, half, issue = fixed[i]
            t, w = free[e]
            for d, h in need[i]:
                h += done[d]
                if h > t:
                    t, w = h, d
            for b in banks:
                k, d, prior = bank[b]
                if k == e:
                    d = prior
                bank[b] = (e, i, d)
                if d >= 0 and done[d] + hop > t:
                    t, w = done[d] + hop, d
            if half == 1:
                if not pool:
                    return None
                b = tile[i] = tile[i + 1] = min(pool, key=pool.get)
                t, w = max((t, w), pool.pop(b))
            if issue:
                free[e] = (t + issue, i)
                t, w = max((t, w), free["d"])
                e = "d"
            why[i] = w
            t += dur[i]
            free[e] = (t, i)
            done[i] = t + lat
            if half == 2:
                pool[tile[i]] = (t + hop, i)
        end = max(done)
        return end + CFG["EVEN"] * max(load.values()), done.index(end), why, tile, end

    def flip(steps):
        for i in steps:
            load[eng[i]] -= dur[i]
            eng[i] = "s" if eng[i] == "v" else "v"
            dur[i] = ops[i]["alt"][eng[i]][1]
            load[eng[i]] += dur[i]

    load = {e: sum(dur[i] for i in range(n) if eng[i] == e) + (2.0 if e == "s" else 0.0) for e in "vs"}
    cur = replay(order)
    best = (cur[0], order, cur[3], list(eng), cur[4])
    rounds = CFG["TRIES"]
    dice = np.random.RandomState(CFG["SEED"]).rand(rounds, 6).tolist()
    for k, (a, b, c, d, e, f) in enumerate(dice):
        slack = -CFG["HEAT"] * (CFG["COLD"] / CFG["HEAT"]) ** (k / rounds) * math.log(1.0 - f)
        chain, i = [], cur[1]
        while cur[2][i] >= 0:
            if cur[2][i] not in ops[i]["deps"]:
                chain.append((cur[2][i], i))
            i = cur[2][i]
        if a < 0.1:
            near = [x for pair in chain for x in pair if "alt" in ops[x]] if b < 0.7 else []
            steps = [(near or flex)[int(c * len(near or flex))]]
            other = flex[int(d * len(flex))]
            steps += [other] * (e < 0.4 and eng[other] != eng[steps[0]])
            flip(steps)
            new, trial = replay(order), order
            if new[0] > cur[0] + slack:
                flip(steps)
                continue
        else:
            if chain and b < 0.8:
                j, i = chain[int(c * len(chain))]
                lo, hi = order.index(j), order.index(i)
            else:
                lo = 3 + int(c * (n - 4))
                hi = min(n - 1, lo + 1 + int(d * 11))
            if lo < 3 or lo >= hi:
                continue
            part = order[lo:hi + 1]
            if e < 0.5:
                move = {part[-1]}
                for x in reversed(part):
                    if x in move:
                        move |= ops[x]["deps"]
                stay = part[0] in move
                part = [x for x in part if x in move] + [x for x in part if x not in move]
            else:
                move = {part[0]}
                for x in part:
                    if ops[x]["deps"] & move:
                        move.add(x)
                stay = part[-1] in move
                part = [x for x in part if x not in move] + [x for x in part if x in move]
            if stay:
                continue
            trial = order[:lo] + part + order[hi + 1:]
            new = replay(trial)
            if new is None or new[0] > cur[0] + slack:
                continue
        order, cur = trial, new
        if cur[0] < best[0]:
            best = (cur[0], order, cur[3], list(eng), cur[4])
    CFG["EST"] = best[4]
    return best[1:4]


def engines(topo, cores):
    sets = [set(topo.engines(a, b)) for a, b in zip(cores, cores[1:] + cores[:1])]
    return sorted(set.intersection(*sets))


def helpers(T, topo, core):
    return [k for k in topo.cores_of(core) if T.rank_of(k) is None and topo.die(k) == topo.die(core)][:CFG["HELP"]]


def plan(T, topo):
    if not PLAN:
        ops = build(None, T, None, 0, None, 0)
        order, tile, takes = schedule(ops)
        names = [ops[i]["sig"][0] for i in order if ops[i]["res"] == "d"]
        folds = [k for k in names if CFG["WAY"][(int(k[2]), int(k[3]))][int(k[4])] in "fF"]
        PLAN.extend([order, tile, folds, takes])
    return PLAN


def hand_on(g, core, T, topo):
    for owner in T.cores:
        mine = helpers(T, topo, owner)
        if core in mine:
            rid, pid, _ = topo.addr(owner)
            n = len(topo.engines(core, owner))
            todo = plan(T, topo)[2][mine.index(core)::len(mine)]
            for name in todo:
                c, s = int(name[2]), int(name[4])
                col = T["cmp%d" % c][:, s * WID:(s + 1) * WID]
                g.wait_ge(T.sem[name], n)
                g.remote_dma(col, col, T.sem[name], T.sem.sent, pid, rid, topo.mask(core, owner))
            if todo:
                g.wait_ge(T.sem.sent, n * len(todo))


def rank_program(g, core, T, topo):
    rank = T.rank_of(core)
    if rank is None:
        hand_on(g, core, T, topo)
        return
    cores = list(T.cores)
    eng = engines(topo, cores)
    mask, narr = sum(1 << x for x in eng), len(eng)
    rid, pid, _ = topo.addr(cores[(rank + 1) % len(cores)])
    order, tile, folds, takes = plan(T, topo)
    mine = helpers(T, topo, core)
    nfold = len(topo.engines(core, mine[0]))

    def send(k, c, r):
        sem = T.sem["%s%d%d" % ({"a": "arr", "m": "mask"}[k], c, r)]
        return g.remote_dma(T["l%s%d%d" % (k, c, r)][:], T["s%s%d%d" % (k, c, r)][:], sem, T.sem.sent, pid, rid, mask)

    def fold(c, r, s, col, a, b):
        name = "ad%d%d%d" % (c, r, s)
        to = mine[folds.index(name) % len(mine)]
        hr, hp, _ = topo.addr(to)
        return g.remote_dma_fused([RemoteDMATransfer(dst_ids=[DstId(rid=hr, pnc=hp)], dma_engine_mask=topo.mask(core, to),
                                                     remote_sem=T.sem[name], srcs=[a, b], dsts=[col], alu_op=1)], local_sem=T.sem.sent)

    ops = build(g, T, send, narr, fold, nfold)
    queue = {"v": g.vector, "s": g.scalar, "p": g.tensor, "g": g, "y": g.sync}
    count = {e: 0 for e in "vspg"}
    seen = {e: {} for e in queue}
    bank = {}

    def wait(e, steps):
        need = {}
        for d in steps:
            sem, val = ops[d]["sig"]
            need[sem] = max(need.get(sem, 0), val)
        for sem in sorted(need):
            if seen[e].get(sem, 0) < need[sem]:
                queue[e].wait_ge(T.sem[sem], need[sem])
                seen[e][sem] = need[sem]

    for i in order:
        o = ops[i]
        e = takes[i]
        if "alt" in o:
            o["calls"] = o["alt"][e][0]
        waits = o["deps"] - o["tardy"]
        args = [T[tile[i]]] if o["tile"] else []
        for b in o["banks"] + ((tile[i],) if o["tile"] else ()):
            waits.update(d for k, d in bank.get(b, {}).items() if k != e)
            bank.setdefault(b, {})[e] = i
        wait(e, waits)
        if o["sig"] is None:
            for k, call in enumerate(o["calls"]):
                if k == o["head"][0]:
                    wait(e, o["tardy"])
                call(*args).then_inc(T.sem[e], 1)
                count[e] += 1
            o["sig"] = (e, count[e])
        elif o["sig"][0].startswith(("arr", "mask")) or o["sig"][0] in folds:
            o["calls"][0]()
        else:
            o["calls"][0]().then_inc(T.sem[o["sig"][0]], 16)
    g.wait_ge(T.sem.sent, narr * 2 * len(CH) * len(RS) + nfold * len(folds))
    for e in "vspg":
        g.wait_ge(T.sem[e], count[e])
    for k in range(4):
        g.sync.wait_ge(T.sem["o%d" % k], 16)
